import numpy as np
import ml_dtypes


def mxq(x, axis, fmt="e4m3"):
    dtype, down = {"e4m3": (ml_dtypes.float8_e4m3fn, 7), "e5m2": (ml_dtypes.float8_e5m2, 14)}[fmt]
    v = np.moveaxis(np.asarray(x, np.float32).astype(ml_dtypes.bfloat16).astype(np.float64), axis, -1)
    blocks = v.reshape(v.shape[:-1] + (-1, 32))
    amax = np.abs(blocks).max(-1, keepdims=True)
    byte = np.maximum(np.where(amax > 0, np.frexp(amax)[1] - 1 + 127, 0) - down, 1)
    scale = np.exp2(byte - 127.0)
    codes = (blocks / scale).astype(np.float32).astype(dtype).astype(np.float64)
    return np.moveaxis((codes * scale).reshape(v.shape), -1, axis)


WIDE = False


def mx_kscale(k):
    if not WIDE:
        return np.ones(k)
    levels = np.array([24, -24, 12, -12, 0])
    if k % 512:
        return np.exp2(np.random.permutation(np.resize(levels, k // 32))).repeat(32)
    a = np.empty((k // 512, 16))
    for p in range(k // 512):
        a[p, :8] = np.random.permutation(np.resize(levels, 8))
        for g in range(8):
            far = levels[np.abs(levels - a[p, g]) >= 10]
            a[p, g + 8] = far[np.random.randint(len(far))]
    return np.exp2(a.ravel()).repeat(32)


def f64(x):
    return np.asarray(x).astype(np.float64)


def striped(idx):
    return np.tile(idx.reshape(-1, 16).T, (8, 1)).astype(np.uint16)


def unstriped(offs):
    return offs[:16].T.reshape(-1).astype(np.int64)


E2M1 = np.array([0.0, 0.5, 1.0, 1.5, 2.0, 3.0, 4.0, 6.0, -0.0, -0.5, -1.0, -1.5, -2.0, -3.0, -4.0, -6.0])


def pack_weight(w, fmt):
    k, n = w.shape
    w = f64(np.asarray(w, np.float32).astype(ml_dtypes.bfloat16)).reshape(k // 32, 32, n)
    amax = np.abs(w).max(1)
    if fmt == "e4m3":
        byte = np.frexp(amax)[1] - 1 + 127 - 7
    else:
        mant, ex = np.frexp(amax / 6.0)
        byte = np.where(mant > 0.5, ex, ex - 1) + 127
    byte = np.clip(np.where(amax > 0, byte, 1), 1, 254)
    scaled = (w * np.exp2(127.0 - byte)[:, None, :]).reshape(k, n).astype(np.float32)
    by_word = np.ascontiguousarray(scaled.reshape(k // 512, 128, 4, n).transpose(0, 1, 3, 2))
    if fmt == "e4m3":
        words = by_word.astype(ml_dtypes.float8_e4m3fn).view(np.uint8)
    else:
        c = by_word.astype(ml_dtypes.float4_e2m1fn).view(np.uint8) & 0xF
        words = (c[..., 0::2] | (c[..., 1::2] << 4)).reshape(k // 512, 128, 2 * n)
    return np.ascontiguousarray(words), np.ascontiguousarray(byte.astype(np.uint8).reshape(k // 512, 16, n))


def unpack_weight(words, scales, fmt):
    g, _, n = scales.shape
    words = np.ascontiguousarray(words).reshape(g, 128, n, -1)
    if fmt == "e4m3":
        vals = words.view(ml_dtypes.float8_e4m3fn).astype(np.float64)
    else:
        nib = np.empty((g, 128, n, 4), np.uint8)
        nib[..., 0::2] = words & 0xF
        nib[..., 1::2] = words >> 4
        vals = E2M1[nib]
    vals = vals * np.repeat(np.exp2(scales.astype(np.float64) - 127.0), 8, axis=1)[..., None]
    return vals.transpose(0, 1, 3, 2).reshape(g * 512, n)


def gelu(f):
    return 0.5 * f * (1.0 + np.tanh(np.sqrt(2.0 / np.pi) * (f + 0.044715 * f**3)))


K, L, N, T, J = 512, 1024, 512, 2048, 512


def setup_inputs():
    n = np.random.standard_normal
    s = mx_kscale(K)[:, None]
    s2 = mx_kscale(L)[:, None]
    p_tab = pack_weight(n((K, T)) * s, "e4m3")
    p_w = pack_weight(n((K, N)) / np.sqrt(K) / s, "e4m3")
    return {
        "tab_words": p_tab[0],
        "tab_scales": p_tab[1],
        "w_words": p_w[0],
        "w_scales": p_w[1],
        "x": (n((L, J)) * s2).astype(np.float32),
        "wx": (n((L, N)) / np.sqrt(L) / s2).astype(np.float32),
        "iw0": (np.random.uniform(0.1, 0.6, J)).astype(np.float32),
        "iw1": (np.random.uniform(0.1, 0.6, J)).astype(np.float32),
        "b": (0.3 * n(N)).astype(np.float32),
        "offs": striped(np.concatenate([np.random.permutation(T)[:J] for _ in range(2)])),
    }


def reference(tab_words, tab_scales, w_words, w_scales, x, wx, iw0, iw1, b, offs):
    idx = unstriped(offs).reshape(2, J)
    tab_ = unpack_weight(tab_words, tab_scales, "e4m3")[:, idx]
    w_ = unpack_weight(w_words, w_scales, "e4m3")
    a0 = w_.T @ tab_[:, 0]
    a1 = w_.T @ tab_[:, 1]
    x_ = mxq(f64(x), 0, "e4m3")
    wx_ = mxq(f64(wx), 0, "e4m3")
    ax = wx_.T @ x_
    return gelu(a0 * f64(iw0)[None, :] + a1 * f64(iw1)[None, :] + ax + f64(b)[:, None])

@@ -1,0 +1,200 @@
+from contextlib import ExitStack
+
+import concourse.mybir as mybir
+from concourse.masks import make_identity
+
+K, L, N, T, J = 512, 1024, 512, 2048, 512
+FLOPS = 2 * N * J * (2 * K + L)
+
+F32 = mybir.dt.float32
+BF16 = mybir.dt.bfloat16
+I32 = mybir.dt.int32
+U32 = mybir.dt.uint32
+U16 = mybir.dt.uint16
+U8 = mybir.dt.uint8
+FP8X4 = mybir.dt.float8_e4m3fn_x4
+ACT = mybir.ActivationFunctionType
+ALU = mybir.AluOpType
+
+P = 128
+PACK = 4
+K_PASS = P * PACK
+BLK = 128
+NB = 4
+XW = 256
+
+
+def tile_list_interp_gelu_kernel(
+    tc, tab_words, tab_scales, w_words, w_scales, x, wx, iw0, iw1, b, offs, out
+):
+    nc = tc.nc
+    with ExitStack() as ctx:
+        keep = ctx.enter_context(tc.tile_pool(name="keep", bufs=1))
+        ring = ctx.enter_context(tc.tile_pool(name="ring", bufs=2))
+        psum_a = ctx.enter_context(tc.psum_pool(name="psum_a", bufs=4))
+        psum_x = ctx.enter_context(tc.psum_pool(name="psum_x", bufs=2))
+        psum_t = ctx.enter_context(tc.psum_pool(name="psum_t", bufs=2))
+
+        offsets = keep.tile([P, 2 * J // 16], U16, name="offsets")
+        tab_w = keep.tile([P, T], I32, name="tab_w", align_bytes=64)
+        tab_s = keep.tile([P, T // 4], I32, name="tab_s", align_bytes=64)
+        w_w = keep.tile([P, N], I32, name="w_w", align_bytes=64)
+        w_s = keep.tile([P, N // 4], I32, name="w_s", align_bytes=64)
+        rows = keep.tile([P, 2, P], F32, name="rows")
+        cols = keep.tile([P, 2 * NB], F32, name="cols")
+        bias = keep.tile([P, NB], F32, name="bias")
+        ident = keep.tile([P, P], F32, name="ident")
+        warm = keep.tile([P, 8], F32, name="warm")
+
+        nc.vector.memset(tab_s[:], 0)
+        nc.vector.memset(w_s[:], 0)
+        nc.gpsimd.memset(rows[:], 0.0)
+        nc.vector.memset(warm[:, 4:8], 0.0)
+
+        def load_scales(queue, plane, scales):
+            src = scales[0].bitcast(I32)
+            for q in range(4):
+                queue.dma_start(out=plane[32 * q : 32 * q + 4, :], in_=src[4 * q : 4 * q + 4, :])
+
+        def load_row(half, r, vec):
+            nc.sync.dma_start(out=rows[r : r + NB, half, :], in_=vec.rearrange("(c p) -> c p", p=P))
+
+        def load_raw(src, a, c0, width, name):
+            raw = keep.tile([P, PACK, width], F32, name=name)
+            nc.sync.dma_start(
+                out=raw[:],
+                in_=src[a * K_PASS : (a + 1) * K_PASS, c0 : c0 + width].rearrange("(p t) c -> p t c", t=PACK),
+            )
+            return raw
+
+        nc.sync.dma_start(offsets[:], offs)
+        tab_src = tab_words[0].rearrange("p n t -> p (n t)").bitcast(I32)
+        x_raw = {}
+        x_raw[0, 0] = load_raw(x, 0, 0, XW, "x_raw00")
+        load_scales(nc.sync, tab_s, tab_scales)
+        load_row(0, 0, iw0)
+        nc.sync.dma_start(out=tab_w[:], in_=tab_src)
+        load_row(0, NB, iw1)
+        make_identity(nc, ident[:])
+        nc.scalar.activation(out=warm[:, 0:1], in_=warm[:, 4:5], func=ACT.Gelu_apprx_tanh)
+
+        x_raw[0, 1] = load_raw(x, 0, XW, XW, "x_raw01")
+        nc.sync.dma_start(out=w_w[:], in_=w_words[0].rearrange("p n t -> p (n t)").bitcast(I32))
+        load_scales(nc.sync, w_s, w_scales)
+        x_raw[1, 0] = load_raw(x, 1, 0, XW, "x_raw10")
+        x_raw[1, 1] = load_raw(x, 1, XW, XW, "x_raw11")
+        load_row(1, 0, b)
+        wx_raw = {}
+        for m in range(NB):
+            for a in range(2):
+                wx_raw[a, m] = load_raw(wx, a, m * BLK, BLK, "wx_raw%d%d" % (a, m))
+
+        got_s, got_w = [], []
+        for g in range(2):
+            gs = keep.tile([P, J], U8, name="got_s%d" % g, align_bytes=64)
+            nc.vector.tensor_copy(gs[:], tab_s[:].bitcast(U8).indirect(offsets[:, g * J // 16 : (g + 1) * J // 16]))
+            got_s.append(gs)
+        for g in range(2):
+            gw = keep.tile([P, J], U32, name="got_w%d" % g, align_bytes=64)
+            nc.vector.tensor_copy(gw[:], tab_w[:].bitcast(U32).indirect(offsets[:, g * J // 16 : (g + 1) * J // 16]))
+            got_w.append(gw)
+
+        vec_t = psum_t.tile([P, J], F32, name="tr")
+        nc.tensor.transpose(vec_t[:, 0:P], rows[:, 0, :], ident[:])
+        nc.scalar.copy(out=cols[:], in_=vec_t[:, 0 : 2 * NB])
+
+        def cast(engine_copy, raw, width, name):
+            grouped = keep.tile([P, width, PACK], BF16, name=name, align_bytes=64)
+            engine_copy(
+                out=grouped[:].rearrange("p (c i) t -> p c t i", i=4),
+                in_=raw[:].rearrange("p t (c i) -> p c t i", i=4),
+            )
+            return grouped
+
+        def quantize(grouped, width, name):
+            codes = keep.tile([P, width], U32, name=name + "_codes", align_bytes=64)
+            scales = keep.tile([P, width], U8, name=name + "_scales", align_bytes=64)
+            nc.vector.quantize_mx(
+                out=codes[:].bitcast(FP8X4), scales=scales[:], in_=grouped[:].rearrange("p c t -> p (c t)")
+            )
+            return codes, scales
+
+        x_q = {}
+        x_g = {}
+        x_g[0, 0] = cast(nc.scalar.copy, x_raw[0, 0], XW, "x_g00")
+        x_g[0, 1] = cast(nc.scalar.copy, x_raw[0, 1], XW, "x_g01")
+        x_q[0, 0] = quantize(x_g[0, 0], XW, "x00")
+        x_q[0, 1] = quantize(x_g[0, 1], XW, "x01")
+
+        u = keep.tile([P, NB, N], F32, name="u")
+        for jb in range(NB):
+            js = slice(jb * BLK, (jb + 1) * BLK)
+            acc = []
+            for g in range(2):
+                a_ps = psum_a.tile([P, N], F32, name="a_ps")
+                nc.tensor.matmul_mx(
+                    out=a_ps[:],
+                    lhsT=got_w[g][:, js].bitcast(FP8X4),
+                    lhsT_scale=got_s[g][:, js],
+                    rhs=w_w[:].bitcast(FP8X4),
+                    rhs_scale=w_s[:].bitcast(U8),
+                    start=True,
+                    stop=True,
+                )
+                acc.append(a_ps)
+            t0 = ring.tile([P, N], F32, name="t0")
+            nc.scalar.activation(out=t0[:], in_=acc[0][:], func=ACT.Copy, scale=cols[:, jb : jb + 1])
+            nc.vector.scalar_tensor_tensor(
+                out=u[:, jb, :],
+                in0=acc[1][:],
+                scalar=cols[:, NB + jb : NB + jb + 1],
+                in1=t0[:],
+                op0=ALU.mult,
+                op1=ALU.add,
+            )
+
+        x_g[1, 0] = cast(nc.vector.tensor_copy, x_raw[1, 0], XW, "x_g10")
+        x_g[1, 1] = cast(nc.scalar.copy, x_raw[1, 1], XW, "x_g11")
+        b_t = psum_t.tile([P, J], F32, name="tr")
+        nc.tensor.transpose(b_t[:, 0:P], rows[:, 1, :], ident[:])
+        nc.scalar.copy(out=bias[:], in_=b_t[:, 0:NB])
+        x_q[1, 0] = quantize(x_g[1, 0], XW, "x10")
+        x_q[1, 1] = quantize(x_g[1, 1], XW, "x11")
+
+        def front(m):
+            g0 = cast(nc.scalar.copy, wx_raw[0, m], BLK, "wx_g0%d" % m)
+            g1 = cast(nc.vector.tensor_copy if m % 2 else nc.scalar.copy, wx_raw[1, m], BLK, "wx_g1%d" % m)
+            wq = [quantize(g0, BLK, "wx0%d" % m), quantize(g1, BLK, "wx1%d" % m)]
+            ax = psum_x.tile([P, NB, BLK], F32, name="ax")
+            for jb in range(NB):
+                h, c0 = divmod(jb * BLK, XW)
+                for a in range(2):
+                    codes, scales = x_q[a, h]
+                    nc.tensor.matmul_mx(
+                        out=ax[:, jb, :],
+                        lhsT=codes[:, c0 : c0 + BLK].bitcast(FP8X4),
+                        lhsT_scale=scales[:, c0 : c0 + BLK],
+                        rhs=wq[a][0][:].bitcast(FP8X4),
+                        rhs_scale=wq[a][1][:],
+                        start=(a == 0),
+                        stop=(a == 1),
+                    )
+            return ax
+
+        def back(m, ax):
+            s = ring.tile([P, NB, BLK], F32, name="s")
+            nc.vector.tensor_tensor(out=s[:], in0=ax[:], in1=u[:, :, m * BLK : (m + 1) * BLK], op=ALU.add)
+            st = psum_t.tile([P, J], F32, name="tr")
+            for jb in range(NB):
+                nc.tensor.transpose(st[:, jb * BLK : (jb + 1) * BLK], s[:, jb, :], ident[:])
+            res = keep.tile([P, J], F32, name="res%d" % m)
+            nc.scalar.activation(
+                out=res[:], in_=st[:], func=ACT.Gelu_apprx_tanh, bias=bias[:, m : m + 1]
+            )
+            nc.sync.dma_start(out=out[m * BLK : (m + 1) * BLK, :], in_=res[:])
+
+        pending = front(0)
+        for m in range(NB):
+            nxt = front(m + 1) if m + 1 < NB else None
+            back(m, pending)
+            pending = nxt

@@ -21,7 +21,37 @@ PACK = 4
 K_PASS = P * PACK
 BLK = 128
 NB = 4
-XW = 256
+
+LOADS = [
+    ("offs",),
+    ("w",),
+    ("iw0",),
+    ("tab_scales", 0),
+    ("tab_scales", 1),
+    ("tab_scales", 2),
+    ("tab_scales", 3),
+    ("tab",),
+    ("iw1",),
+    ("wx", 0, 0, 2),
+    ("w_scales", 0),
+    ("w_scales", 1),
+    ("w_scales", 2),
+    ("w_scales", 3),
+    ("x", 1, 0, 2),
+    ("b",),
+    ("x", 0, 0, 4),
+    ("wx", 1, 0, 2),
+    ("x", 1, 2, 2),
+    ("wx", 1, 2, 1),
+    ("wx", 0, 2, 1),
+    ("wx", 0, 3, 1),
+    ("wx", 1, 3, 1),
+]
+ON_VECTOR = {("x", 0, 3), ("x", 1, 0), ("x", 1, 1), ("x", 1, 3), ("wx", 1, 0), ("wx", 1, 2)}
+WORD_GATHERS = 2
+SCALE_GATHERS = 1
+DEPTH = 4
+PIECES = [2, 1, 1, 2]
 
 
 def tile_list_interp_gelu_kernel(
@@ -30,10 +60,10 @@ def tile_list_interp_gelu_kernel(
     nc = tc.nc
     with ExitStack() as ctx:
         keep = ctx.enter_context(tc.tile_pool(name="keep", bufs=1))
-        ring = ctx.enter_context(tc.tile_pool(name="ring", bufs=2))
-        psum_a = ctx.enter_context(tc.psum_pool(name="psum_a", bufs=4))
-        psum_x = ctx.enter_context(tc.psum_pool(name="psum_x", bufs=2))
-        psum_t = ctx.enter_context(tc.psum_pool(name="psum_t", bufs=2))
+        psum = ctx.enter_context(tc.psum_pool(name="psum", bufs=1))
+
+        def bank(i):
+            return psum.tile([P, NB, BLK], F32, name="bank%d" % i)
 
         offsets = keep.tile([P, 2 * J // 16], U16, name="offsets")
         tab_w = keep.tile([P, T], I32, name="tab_w", align_bytes=64)
@@ -51,150 +81,176 @@ def tile_list_interp_gelu_kernel(
         nc.gpsimd.memset(rows[:], 0.0)
         nc.vector.memset(warm[:, 4:8], 0.0)
 
-        def load_scales(queue, plane, scales):
-            src = scales[0].bitcast(I32)
-            for q in range(4):
-                queue.dma_start(out=plane[32 * q : 32 * q + 4, :], in_=src[4 * q : 4 * q + 4, :])
+        raw = {}
+        for item in LOADS:
+            kind = item[0]
+            if kind == "offs":
+                nc.sync.dma_start(offsets[:], offs)
+            elif kind in ("tab", "w"):
+                dst, src = (tab_w, tab_words) if kind == "tab" else (w_w, w_words)
+                nc.sync.dma_start(out=dst[:], in_=src[0].rearrange("p n t -> p (n t)").bitcast(I32))
+            elif kind in ("tab_scales", "w_scales"):
+                dst, src = (tab_s, tab_scales) if kind == "tab_scales" else (w_s, w_scales)
+                q = item[1]
+                nc.sync.dma_start(out=dst[q:P:32, :], in_=src[0].bitcast(I32)[q:16:4, :])
+            elif kind in ("iw0", "iw1", "b"):
+                vec, half, r = {"iw0": (iw0, 0, 0), "iw1": (iw1, 0, NB), "b": (b, 1, 0)}[kind]
+                nc.sync.dma_start(out=rows[r : r + NB, half, :], in_=vec.rearrange("(c p) -> c p", p=P))
+            else:
+                a, first, count = item[1:]
+                src = x if kind == "x" else wx
+                chunk = keep.tile([P, PACK, count * BLK], F32, name="raw_%s%d%d" % (kind, a, first))
+                nc.sync.dma_start(
+                    out=chunk[:],
+                    in_=src[a * K_PASS : (a + 1) * K_PASS, first * BLK : (first + count) * BLK].rearrange(
+                        "(p t) c -> p t c", t=PACK
+                    ),
+                )
+                for i in range(count):
+                    raw[kind, a, first + i] = chunk, i
 
-        def load_row(half, r, vec):
-            nc.sync.dma_start(out=rows[r : r + NB, half, :], in_=vec.rearrange("(c p) -> c p", p=P))
-
-        def load_raw(src, a, c0, width, name):
-            raw = keep.tile([P, PACK, width], F32, name=name)
-            nc.sync.dma_start(
-                out=raw[:],
-                in_=src[a * K_PASS : (a + 1) * K_PASS, c0 : c0 + width].rearrange("(p t) c -> p t c", t=PACK),
-            )
-            return raw
-
-        nc.sync.dma_start(offsets[:], offs)
-        tab_src = tab_words[0].rearrange("p n t -> p (n t)").bitcast(I32)
-        x_raw = {}
-        x_raw[0, 0] = load_raw(x, 0, 0, XW, "x_raw00")
-        load_scales(nc.sync, tab_s, tab_scales)
-        load_row(0, 0, iw0)
-        nc.sync.dma_start(out=tab_w[:], in_=tab_src)
-        load_row(0, NB, iw1)
         make_identity(nc, ident[:])
         nc.scalar.activation(out=warm[:, 0:1], in_=warm[:, 4:5], func=ACT.Gelu_apprx_tanh)
 
-        x_raw[0, 1] = load_raw(x, 0, XW, XW, "x_raw01")
-        nc.sync.dma_start(out=w_w[:], in_=w_words[0].rearrange("p n t -> p (n t)").bitcast(I32))
-        load_scales(nc.sync, w_s, w_scales)
-        x_raw[1, 0] = load_raw(x, 1, 0, XW, "x_raw10")
-        x_raw[1, 1] = load_raw(x, 1, XW, XW, "x_raw11")
-        load_row(1, 0, b)
-        wx_raw = {}
-        for m in range(NB):
-            for a in range(2):
-                wx_raw[a, m] = load_raw(wx, a, m * BLK, BLK, "wx_raw%d%d" % (a, m))
+        got_s = keep.tile([P, 2 * J], U8, name="got_s", align_bytes=64)
+        got_w = keep.tile([P, 2 * J], U32, name="got_w", align_bytes=64)
+        for got, window, pieces in (
+            (got_s, tab_s[:].bitcast(U8), SCALE_GATHERS),
+            (got_w, tab_w[:].bitcast(U32), 2 * WORD_GATHERS),
+        ):
+            width = 2 * J // pieces
+            for i in range(pieces):
+                nc.vector.tensor_copy(
+                    got[:, i * width : (i + 1) * width],
+                    window.indirect(offsets[:, i * width // 16 : (i + 1) * width // 16]),
+                )
 
-        got_s, got_w = [], []
-        for g in range(2):
-            gs = keep.tile([P, J], U8, name="got_s%d" % g, align_bytes=64)
-            nc.vector.tensor_copy(gs[:], tab_s[:].bitcast(U8).indirect(offsets[:, g * J // 16 : (g + 1) * J // 16]))
-            got_s.append(gs)
-        for g in range(2):
-            gw = keep.tile([P, J], U32, name="got_w%d" % g, align_bytes=64)
-            nc.vector.tensor_copy(gw[:], tab_w[:].bitcast(U32).indirect(offsets[:, g * J // 16 : (g + 1) * J // 16]))
-            got_w.append(gw)
+        vec_t = bank(7)
+        nc.tensor.transpose(vec_t[:, 0, :], rows[:, 0, :], ident[:])
+        nc.scalar.copy(out=cols[:], in_=vec_t[:, 0, 0 : 2 * NB])
+        b_t = bank(7)
+        nc.tensor.transpose(b_t[:, 0, :], rows[:, 1, :], ident[:])
+        nc.scalar.copy(out=bias[:], in_=b_t[:, 0, 0:NB])
 
-        vec_t = psum_t.tile([P, J], F32, name="tr")
-        nc.tensor.transpose(vec_t[:, 0:P], rows[:, 0, :], ident[:])
-        nc.scalar.copy(out=cols[:], in_=vec_t[:, 0 : 2 * NB])
-
-        def cast(engine_copy, raw, width, name):
-            grouped = keep.tile([P, width, PACK], BF16, name=name, align_bytes=64)
-            engine_copy(
-                out=grouped[:].rearrange("p (c i) t -> p c t i", i=4),
-                in_=raw[:].rearrange("p t (c i) -> p c t i", i=4),
+        def cast(grouped, key):
+            copy = nc.vector.tensor_copy if key in ON_VECTOR else nc.scalar.copy
+            chunk, i = raw[key]
+            src = chunk[:, :, i * BLK : i * BLK + grouped.shape[1]]
+            copy(
+                out=grouped.rearrange("p (c i) t -> p c t i", i=4),
+                in_=src.rearrange("p t (c i) -> p c t i", i=4),
             )
-            return grouped
 
-        def quantize(grouped, width, name):
+        def quantize(grouped, name):
+            width = grouped.shape[1]
             codes = keep.tile([P, width], U32, name=name + "_codes", align_bytes=64)
             scales = keep.tile([P, width], U8, name=name + "_scales", align_bytes=64)
             nc.vector.quantize_mx(
-                out=codes[:].bitcast(FP8X4), scales=scales[:], in_=grouped[:].rearrange("p c t -> p (c t)")
+                out=codes[:].bitcast(FP8X4), scales=scales[:], in_=grouped.rearrange("p c t -> p (c t)")
             )
             return codes, scales
 
-        x_q = {}
-        x_g = {}
-        x_g[0, 0] = cast(nc.scalar.copy, x_raw[0, 0], XW, "x_g00")
-        x_g[0, 1] = cast(nc.scalar.copy, x_raw[0, 1], XW, "x_g01")
-        x_q[0, 0] = quantize(x_g[0, 0], XW, "x00")
-        x_q[0, 1] = quantize(x_g[0, 1], XW, "x01")
+        x_g, x_q = {}, {}
+
+        def cast_x(a):
+            for h in range(2):
+                x_g[a, h] = keep.tile([P, 2 * BLK, PACK], BF16, name="x_g%d%d" % (a, h), align_bytes=64)
+                k0, k1 = ("x", a, 2 * h), ("x", a, 2 * h + 1)
+                if (k0 in ON_VECTOR) == (k1 in ON_VECTOR) and raw[k1][1] == raw[k0][1] + 1:
+                    cast(x_g[a, h][:], k0)
+                else:
+                    cast(x_g[a, h][:, :BLK, :], k0)
+                    cast(x_g[a, h][:, BLK:, :], k1)
+
+        def quantize_x(a):
+            for h in range(2):
+                x_q[a, h] = quantize(x_g[a, h][:], "x%d%d" % (a, h))
 
         u = keep.tile([P, NB, N], F32, name="u")
-        for jb in range(NB):
-            js = slice(jb * BLK, (jb + 1) * BLK)
-            acc = []
-            for g in range(2):
-                a_ps = psum_a.tile([P, N], F32, name="a_ps")
-                nc.tensor.matmul_mx(
-                    out=a_ps[:],
-                    lhsT=got_w[g][:, js].bitcast(FP8X4),
-                    lhsT_scale=got_s[g][:, js],
-                    rhs=w_w[:].bitcast(FP8X4),
-                    rhs_scale=w_s[:].bitcast(U8),
-                    start=True,
-                    stop=True,
-                )
-                acc.append(a_ps)
-            t0 = ring.tile([P, N], F32, name="t0")
-            nc.scalar.activation(out=t0[:], in_=acc[0][:], func=ACT.Copy, scale=cols[:, jb : jb + 1])
+
+        def project(g, jb):
+            js = slice(g * J + jb * BLK, g * J + (jb + 1) * BLK)
+            acc = bank(NB * g + jb)
+            nc.tensor.matmul_mx(
+                out=acc[:].rearrange("p c n -> p (c n)"),
+                lhsT=got_w[:, js].bitcast(FP8X4),
+                lhsT_scale=got_s[:, js],
+                rhs=w_w[:].bitcast(FP8X4),
+                rhs_scale=w_s[:].bitcast(U8),
+                start=True,
+                stop=True,
+            )
+            return acc[:].rearrange("p c n -> p (c n)")
+
+        def weigh0(jb, acc):
+            t0 = keep.tile([P, N], F32, name="t0_%d" % jb)
+            nc.scalar.activation(out=t0[:], in_=acc, func=ACT.Copy, scale=cols[:, jb : jb + 1])
+            return t0
+
+        def weigh1(jb, acc, t0):
             nc.vector.scalar_tensor_tensor(
                 out=u[:, jb, :],
-                in0=acc[1][:],
+                in0=acc,
                 scalar=cols[:, NB + jb : NB + jb + 1],
                 in1=t0[:],
                 op0=ALU.mult,
                 op1=ALU.add,
             )
 
-        x_g[1, 0] = cast(nc.vector.tensor_copy, x_raw[1, 0], XW, "x_g10")
-        x_g[1, 1] = cast(nc.scalar.copy, x_raw[1, 1], XW, "x_g11")
-        b_t = psum_t.tile([P, J], F32, name="tr")
-        nc.tensor.transpose(b_t[:, 0:P], rows[:, 1, :], ident[:])
-        nc.scalar.copy(out=bias[:], in_=b_t[:, 0:NB])
-        x_q[1, 0] = quantize(x_g[1, 0], XW, "x10")
-        x_q[1, 1] = quantize(x_g[1, 1], XW, "x11")
+        def interpolate():
+            t0 = [weigh0(jb, project(0, jb)) for jb in range(NB)]
+            for jb in range(NB):
+                weigh1(jb, project(1, jb), t0[jb])
+
+        cast_x(0)
+        quantize_x(0)
+        interpolate()
+        cast_x(1)
+        quantize_x(1)
 
         def front(m):
-            g0 = cast(nc.scalar.copy, wx_raw[0, m], BLK, "wx_g0%d" % m)
-            g1 = cast(nc.vector.tensor_copy if m % 2 else nc.scalar.copy, wx_raw[1, m], BLK, "wx_g1%d" % m)
-            wq = [quantize(g0, BLK, "wx0%d" % m), quantize(g1, BLK, "wx1%d" % m)]
-            ax = psum_x.tile([P, NB, BLK], F32, name="ax")
+            grouped = keep.tile([P, 2 * BLK, PACK], BF16, name="wx_g%d" % m, align_bytes=64)
+            for a in range(2):
+                cast(grouped[:, a * BLK : (a + 1) * BLK, :], ("wx", a, m))
+            wq = [quantize(grouped[:, a * BLK : (a + 1) * BLK, :], "wx%d%d" % (a, m)) for a in range(2)]
+            wq = [(codes[:], scales[:]) for codes, scales in wq]
+            ax = bank(m)
             for jb in range(NB):
-                h, c0 = divmod(jb * BLK, XW)
+                h, i = divmod(jb, 2)
                 for a in range(2):
                     codes, scales = x_q[a, h]
                     nc.tensor.matmul_mx(
                         out=ax[:, jb, :],
-                        lhsT=codes[:, c0 : c0 + BLK].bitcast(FP8X4),
-                        lhsT_scale=scales[:, c0 : c0 + BLK],
-                        rhs=wq[a][0][:].bitcast(FP8X4),
-                        rhs_scale=wq[a][1][:],
+                        lhsT=codes[:, i * BLK : (i + 1) * BLK].bitcast(FP8X4),
+                        lhsT_scale=scales[:, i * BLK : (i + 1) * BLK],
+                        rhs=wq[a][0].bitcast(FP8X4),
+                        rhs_scale=wq[a][1],
                         start=(a == 0),
                         stop=(a == 1),
                     )
             return ax
 
-        def back(m, ax):
-            s = ring.tile([P, NB, BLK], F32, name="s")
-            nc.vector.tensor_tensor(out=s[:], in0=ax[:], in1=u[:, :, m * BLK : (m + 1) * BLK], op=ALU.add)
-            st = psum_t.tile([P, J], F32, name="tr")
-            for jb in range(NB):
-                nc.tensor.transpose(st[:, jb * BLK : (jb + 1) * BLK], s[:, jb, :], ident[:])
-            res = keep.tile([P, J], F32, name="res%d" % m)
-            nc.scalar.activation(
-                out=res[:], in_=st[:], func=ACT.Gelu_apprx_tanh, bias=bias[:, m : m + 1]
-            )
-            nc.sync.dma_start(out=out[m * BLK : (m + 1) * BLK, :], in_=res[:])
+        free_banks = [4, 5, 6, 7, 0, 1]
 
-        pending = front(0)
+        def back(m, ax):
+            count = NB // PIECES[m]
+            for first in range(0, NB, count):
+                jbs = slice(first, first + count)
+                s = sums[:, m, jbs, :]
+                nc.vector.tensor_tensor(out=s, in0=ax[:, jbs, :], in1=u[:, jbs, m * BLK : (m + 1) * BLK], op=ALU.add)
+                st = bank(free_banks[sum(PIECES[:m]) + first // count])
+                for i in range(count):
+                    nc.tensor.transpose(st[:, i, :], s[:, i, :], ident[:])
+                res = keep.tile([P, count, BLK], F32, name="res%d%d" % (m, first))
+                nc.scalar.activation(
+                    out=res[:], in_=st[:, 0:count, :], func=ACT.Gelu_apprx_tanh, bias=bias[:, m : m + 1]
+                )
+                nc.sync.dma_start(
+                    out=out[m * BLK : (m + 1) * BLK, first * BLK : (first + count) * BLK],
+                    in_=res[:].rearrange("p c n -> p (c n)"),
+                )
+
+        pending = [front(m) for m in range(DEPTH)]
+        sums = keep.tile([P, NB, NB, BLK], F32, name="sums", tag="wx_g%d" % (NB - 1), align_bytes=64)
         for m in range(NB):
-            nxt = front(m + 1) if m + 1 < NB else None
-            back(m, pending)
-            pending = nxt
+            back(m, pending[m])

@@ -25,33 +25,35 @@ NB = 4
 LOADS = [
     ("offs",),
     ("w",),
-    ("iw0",),
     ("tab_scales", 0),
+    ("w_scales", 0),
     ("tab_scales", 1),
     ("tab_scales", 2),
     ("tab_scales", 3),
     ("tab",),
-    ("iw1",),
-    ("wx", 0, 0, 2),
-    ("w_scales", 0),
     ("w_scales", 1),
+    ("iw0",),
+    ("b",),
+    ("iw1",),
+    ("x", 0, 0, 2),
     ("w_scales", 2),
     ("w_scales", 3),
+    ("wx", 0, 1, 1),
     ("x", 1, 0, 2),
-    ("b",),
-    ("x", 0, 0, 4),
-    ("wx", 1, 0, 2),
-    ("x", 1, 2, 2),
-    ("wx", 1, 2, 1),
+    ("wx", 0, 0, 1),
+    ("x", 0, 2, 2),
+    ("x", 1, 3, 1),
+    ("x", 1, 2, 1),
+    ("wx", 1, 0, 3),
     ("wx", 0, 2, 1),
     ("wx", 0, 3, 1),
     ("wx", 1, 3, 1),
 ]
-ON_VECTOR = {("x", 0, 3), ("x", 1, 0), ("x", 1, 1), ("x", 1, 3), ("wx", 1, 0), ("wx", 1, 2)}
+ON_VECTOR = {("x", 1, 0), ("x", 1, 1), ("wx", 1, 0), ("wx", 0, 1), ("wx", 1, 1), ("wx", 0, 2), ("wx", 1, 2)}
 WORD_GATHERS = 2
 SCALE_GATHERS = 1
 DEPTH = 4
-PIECES = [2, 1, 1, 2]
+PIECES = [1, 1, 1, 2]
 
 
 def tile_list_interp_gelu_kernel(
@@ -70,9 +72,8 @@ def tile_list_interp_gelu_kernel(
         tab_s = keep.tile([P, T // 4], I32, name="tab_s", align_bytes=64)
         w_w = keep.tile([P, N], I32, name="w_w", align_bytes=64)
         w_s = keep.tile([P, N // 4], I32, name="w_s", align_bytes=64)
-        rows = keep.tile([P, 2, P], F32, name="rows")
-        cols = keep.tile([P, 2 * NB], F32, name="cols")
-        bias = keep.tile([P, NB], F32, name="bias")
+        rows = keep.tile([P, 1, P], F32, name="rows")
+        cols = keep.tile([P, 3 * NB], F32, name="cols")
         ident = keep.tile([P, P], F32, name="ident")
         warm = keep.tile([P, 8], F32, name="warm")
 
@@ -94,7 +95,7 @@ def tile_list_interp_gelu_kernel(
                 q = item[1]
                 nc.sync.dma_start(out=dst[q:P:32, :], in_=src[0].bitcast(I32)[q:16:4, :])
             elif kind in ("iw0", "iw1", "b"):
-                vec, half, r = {"iw0": (iw0, 0, 0), "iw1": (iw1, 0, NB), "b": (b, 1, 0)}[kind]
+                vec, half, r = {"iw0": (iw0, 0, 0), "iw1": (iw1, 0, NB), "b": (b, 0, 2 * NB)}[kind]
                 nc.sync.dma_start(out=rows[r : r + NB, half, :], in_=vec.rearrange("(c p) -> c p", p=P))
             else:
                 a, first, count = item[1:]
@@ -127,10 +128,8 @@ def tile_list_interp_gelu_kernel(
 
         vec_t = bank(7)
         nc.tensor.transpose(vec_t[:, 0, :], rows[:, 0, :], ident[:])
-        nc.scalar.copy(out=cols[:], in_=vec_t[:, 0, 0 : 2 * NB])
-        b_t = bank(7)
-        nc.tensor.transpose(b_t[:, 0, :], rows[:, 1, :], ident[:])
-        nc.scalar.copy(out=bias[:], in_=b_t[:, 0, 0:NB])
+        nc.scalar.copy(out=cols[:], in_=vec_t[:, 0, 0 : 3 * NB])
+        bias = cols[:, 2 * NB :]
 
         def cast(grouped, key):
             copy = nc.vector.tensor_copy if key in ON_VECTOR else nc.scalar.copy
@@ -163,8 +162,16 @@ def tile_list_interp_gelu_kernel(
                     cast(x_g[a, h][:, BLK:, :], k1)
 
         def quantize_x(a):
+            codes = keep.tile([P, J], U32, name="x%d_codes" % a, align_bytes=64)
+            scales = keep.tile([P, J], U8, name="x%d_scales" % a, align_bytes=64)
             for h in range(2):
-                x_q[a, h] = quantize(x_g[a, h][:], "x%d%d" % (a, h))
+                half = slice(h * J // 2, (h + 1) * J // 2)
+                nc.vector.quantize_mx(
+                    out=codes[:, half].bitcast(FP8X4),
+                    scales=scales[:, half],
+                    in_=x_g[a, h][:].rearrange("p c t -> p (c t)"),
+                )
+            x_q[a] = codes, scales
 
         u = keep.tile([P, NB, N], F32, name="u")
 
@@ -208,49 +215,47 @@ def tile_list_interp_gelu_kernel(
         cast_x(1)
         quantize_x(1)
 
+        u_t = []
+        for m in range(NB):
+            turned = bank(m)
+            for jb in range(NB):
+                nc.tensor.transpose(turned[:, jb, :], u[:, jb, m * BLK : (m + 1) * BLK], ident[:])
+            u_m = keep.tile([P, J], F32, name="u_t%d" % m)
+            copy = nc.vector.tensor_copy if m in [] else nc.scalar.copy
+            copy(out=u_m[:], in_=turned[:].rearrange("p c n -> p (c n)"))
+            u_t.append(u_m)
+
         def front(m):
             grouped = keep.tile([P, 2 * BLK, PACK], BF16, name="wx_g%d" % m, align_bytes=64)
             for a in range(2):
                 cast(grouped[:, a * BLK : (a + 1) * BLK, :], ("wx", a, m))
             wq = [quantize(grouped[:, a * BLK : (a + 1) * BLK, :], "wx%d%d" % (a, m)) for a in range(2)]
             wq = [(codes[:], scales[:]) for codes, scales in wq]
-            ax = bank(m)
-            for jb in range(NB):
-                h, i = divmod(jb, 2)
-                for a in range(2):
-                    codes, scales = x_q[a, h]
-                    nc.tensor.matmul_mx(
-                        out=ax[:, jb, :],
-                        lhsT=codes[:, i * BLK : (i + 1) * BLK].bitcast(FP8X4),
-                        lhsT_scale=scales[:, i * BLK : (i + 1) * BLK],
-                        rhs=wq[a][0].bitcast(FP8X4),
-                        rhs_scale=wq[a][1],
-                        start=(a == 0),
-                        stop=(a == 1),
-                    )
+            ax_bank = bank(NB + m)
+            ax = ax_bank[:].rearrange("p c n -> p (c n)")
+            for a in range(2):
+                nc.tensor.matmul_mx(
+                    out=ax,
+                    lhsT=wq[a][0].bitcast(FP8X4),
+                    lhsT_scale=wq[a][1],
+                    rhs=x_q[a][0][:].bitcast(FP8X4),
+                    rhs_scale=x_q[a][1][:],
+                    start=(a == 0),
+                    stop=(a == 1),
+                )
             return ax
 
-        free_banks = [4, 5, 6, 7, 0, 1]
-
         def back(m, ax):
-            count = NB // PIECES[m]
-            for first in range(0, NB, count):
-                jbs = slice(first, first + count)
-                s = sums[:, m, jbs, :]
-                nc.vector.tensor_tensor(out=s, in0=ax[:, jbs, :], in1=u[:, jbs, m * BLK : (m + 1) * BLK], op=ALU.add)
-                st = bank(free_banks[sum(PIECES[:m]) + first // count])
-                for i in range(count):
-                    nc.tensor.transpose(st[:, i, :], s[:, i, :], ident[:])
-                res = keep.tile([P, count, BLK], F32, name="res%d%d" % (m, first))
-                nc.scalar.activation(
-                    out=res[:], in_=st[:, 0:count, :], func=ACT.Gelu_apprx_tanh, bias=bias[:, m : m + 1]
-                )
-                nc.sync.dma_start(
-                    out=out[m * BLK : (m + 1) * BLK, first * BLK : (first + count) * BLK],
-                    in_=res[:].rearrange("p c n -> p (c n)"),
-                )
+            width = J // PIECES[m]
+            for j0 in range(0, J, width):
+                js = slice(j0, j0 + width)
+                s = sums[:, m, :, :].rearrange("p c n -> p (c n)")[:, js]
+                nc.vector.tensor_tensor(out=s, in0=ax[:, js], in1=u_t[m][:, js], op=ALU.add)
+                res = keep.tile([P, width], F32, name="res%d_%d" % (m, j0))
+                nc.scalar.activation(out=res[:], in_=s, func=ACT.Gelu_apprx_tanh, bias=bias[:, m : m + 1])
+                nc.sync.dma_start(out=out[m * BLK : (m + 1) * BLK, js], in_=res[:])
 
         pending = [front(m) for m in range(DEPTH)]
-        sums = keep.tile([P, NB, NB, BLK], F32, name="sums", tag="wx_g%d" % (NB - 1), align_bytes=64)
+        sums = keep.tile([P, NB, NB, BLK], F32, name="sums", tag="wx_g1", align_bytes=64)
         for m in range(NB):
             back(m, pending[m])

@@ -19,41 +19,11 @@ ALU = mybir.AluOpType
 P = 128
 PACK = 4
 K_PASS = P * PACK
+PASSES = L // K_PASS
 BLK = 128
 NB = 4
-
-LOADS = [
-    ("offs",),
-    ("w",),
-    ("tab_scales", 0),
-    ("w_scales", 0),
-    ("tab_scales", 1),
-    ("tab_scales", 2),
-    ("tab_scales", 3),
-    ("tab",),
-    ("w_scales", 1),
-    ("iw0",),
-    ("b",),
-    ("iw1",),
-    ("x", 0, 0, 2),
-    ("w_scales", 2),
-    ("w_scales", 3),
-    ("wx", 0, 1, 1),
-    ("x", 1, 0, 2),
-    ("wx", 0, 0, 1),
-    ("x", 0, 2, 2),
-    ("x", 1, 3, 1),
-    ("x", 1, 2, 1),
-    ("wx", 1, 0, 3),
-    ("wx", 0, 2, 1),
-    ("wx", 0, 3, 1),
-    ("wx", 1, 3, 1),
-]
-ON_VECTOR = {("x", 1, 0), ("x", 1, 1), ("wx", 1, 0), ("wx", 0, 1), ("wx", 1, 1), ("wx", 0, 2), ("wx", 1, 2)}
-WORD_GATHERS = 2
-SCALE_GATHERS = 1
-DEPTH = 4
-PIECES = [1, 1, 1, 2]
+HALF = 256
+TURNED = 2
 
 
 def tile_list_interp_gelu_kernel(
@@ -67,195 +37,183 @@ def tile_list_interp_gelu_kernel(
         def bank(i):
             return psum.tile([P, NB, BLK], F32, name="bank%d" % i)
 
+        def flat(tile):
+            return tile[:].rearrange("p c n -> p (c n)")
+
         offsets = keep.tile([P, 2 * J // 16], U16, name="offsets")
         tab_w = keep.tile([P, T], I32, name="tab_w", align_bytes=64)
         tab_s = keep.tile([P, T // 4], I32, name="tab_s", align_bytes=64)
         w_w = keep.tile([P, N], I32, name="w_w", align_bytes=64)
         w_s = keep.tile([P, N // 4], I32, name="w_s", align_bytes=64)
-        rows = keep.tile([P, 1, P], F32, name="rows")
-        cols = keep.tile([P, 3 * NB], F32, name="cols")
+        iw_rows = keep.tile([P, P], F32, name="iw_rows")
+        b_rows = keep.tile([P, P], F32, name="b_rows")
+        iw_cols = keep.tile([P, 2 * NB], F32, name="iw_cols")
+        b_cols = keep.tile([P, NB], F32, name="b_cols")
         ident = keep.tile([P, P], F32, name="ident")
         warm = keep.tile([P, 8], F32, name="warm")
 
         nc.vector.memset(tab_s[:], 0)
+        nc.vector.memset(iw_rows[:], 0.0)
         nc.vector.memset(w_s[:], 0)
-        nc.gpsimd.memset(rows[:], 0.0)
-        nc.vector.memset(warm[:, 4:8], 0.0)
-
-        raw = {}
-        for item in LOADS:
-            kind = item[0]
-            if kind == "offs":
-                nc.sync.dma_start(offsets[:], offs)
-            elif kind in ("tab", "w"):
-                dst, src = (tab_w, tab_words) if kind == "tab" else (w_w, w_words)
-                nc.sync.dma_start(out=dst[:], in_=src[0].rearrange("p n t -> p (n t)").bitcast(I32))
-            elif kind in ("tab_scales", "w_scales"):
-                dst, src = (tab_s, tab_scales) if kind == "tab_scales" else (w_s, w_scales)
-                q = item[1]
-                nc.sync.dma_start(out=dst[q:P:32, :], in_=src[0].bitcast(I32)[q:16:4, :])
-            elif kind in ("iw0", "iw1", "b"):
-                vec, half, r = {"iw0": (iw0, 0, 0), "iw1": (iw1, 0, NB), "b": (b, 0, 2 * NB)}[kind]
-                nc.sync.dma_start(out=rows[r : r + NB, half, :], in_=vec.rearrange("(c p) -> c p", p=P))
-            else:
-                a, first, count = item[1:]
-                src = x if kind == "x" else wx
-                chunk = keep.tile([P, PACK, count * BLK], F32, name="raw_%s%d%d" % (kind, a, first))
-                nc.sync.dma_start(
-                    out=chunk[:],
-                    in_=src[a * K_PASS : (a + 1) * K_PASS, first * BLK : (first + count) * BLK].rearrange(
-                        "(p t) c -> p t c", t=PACK
-                    ),
-                )
-                for i in range(count):
-                    raw[kind, a, first + i] = chunk, i
-
+        nc.vector.memset(b_rows[:], 0.0)
         make_identity(nc, ident[:])
-        nc.scalar.activation(out=warm[:, 0:1], in_=warm[:, 4:5], func=ACT.Gelu_apprx_tanh)
+
+        def load_words(dst, src):
+            nc.sync.dma_start(out=dst[:], in_=src[0].rearrange("p n t -> p (n t)").bitcast(I32))
+
+        def load_scales(queue, dst, src, r):
+            queue.dma_start(out=dst[r:P:32, :], in_=src[0].bitcast(I32)[r:16:4, :])
+
+        def load_vector(queue, rows, i, vec):
+            queue.dma_start(out=rows[i * NB : (i + 1) * NB, :], in_=vec.rearrange("(c p) -> c p", p=P))
+
+        def load_rows(src, a, first, width, name):
+            chunk = keep.tile([P, PACK, width], F32, name=name)
+            nc.sync.dma_start(
+                out=chunk[:],
+                in_=src[a * K_PASS : (a + 1) * K_PASS, first : first + width].rearrange("(p t) c -> p t c", t=PACK),
+            )
+            return chunk
+
+        nc.sync.dma_start(offsets[:], offs)
+        load_words(w_w, w_words)
+        for r in range(4):
+            load_scales(nc.sync if r < 3 else nc.scalar, tab_s, tab_scales, r)
+        nc.scalar.activation(out=warm[:, 0:1], in_=b_rows[:, 0:1], func=ACT.Gelu_apprx_tanh)
+        load_words(tab_w, tab_words)
+        load_vector(nc.sync, iw_rows, 0, iw0)
+        load_vector(nc.sync, iw_rows, 1, iw1)
+        for r in range(4):
+            load_scales(nc.sync, w_s, w_scales, r)
+        x_raw = [load_rows(x, 0, 0, J, "x_raw0")]
+        load_vector(nc.sync, b_rows, 0, b)
+        x_raw.append(load_rows(x, 1, 0, J, "x_raw1"))
+        wx_raw = [[load_rows(wx, a, m * BLK, BLK, "wx_raw%d%d" % (m, a)) for a in range(PASSES)] for m in range(NB)]
 
         got_s = keep.tile([P, 2 * J], U8, name="got_s", align_bytes=64)
         got_w = keep.tile([P, 2 * J], U32, name="got_w", align_bytes=64)
-        for got, window, pieces in (
-            (got_s, tab_s[:].bitcast(U8), SCALE_GATHERS),
-            (got_w, tab_w[:].bitcast(U32), 2 * WORD_GATHERS),
-        ):
-            width = 2 * J // pieces
-            for i in range(pieces):
-                nc.vector.tensor_copy(
-                    got[:, i * width : (i + 1) * width],
-                    window.indirect(offsets[:, i * width // 16 : (i + 1) * width // 16]),
-                )
+        nc.vector.tensor_copy(got_s[:], tab_s[:].bitcast(U8).indirect(offsets[:]))
+        for i in range(2 * J // HALF):
+            nc.vector.tensor_copy(
+                got_w[:, i * HALF : (i + 1) * HALF],
+                tab_w[:].bitcast(U32).indirect(offsets[:, i * HALF // 16 : (i + 1) * HALF // 16]),
+            )
 
-        vec_t = bank(7)
-        nc.tensor.transpose(vec_t[:, 0, :], rows[:, 0, :], ident[:])
-        nc.scalar.copy(out=cols[:], in_=vec_t[:, 0, 0 : 3 * NB])
-        bias = cols[:, 2 * NB :]
+        def to_columns(cols, rows, turned):
+            nc.tensor.transpose(turned[:, 0, :], rows[:], ident[:])
+            nc.scalar.copy(out=cols[:], in_=turned[:, 0, 0 : cols.shape[1]])
 
-        def cast(grouped, key):
-            copy = nc.vector.tensor_copy if key in ON_VECTOR else nc.scalar.copy
-            chunk, i = raw[key]
-            src = chunk[:, :, i * BLK : i * BLK + grouped.shape[1]]
+        to_columns(iw_cols, iw_rows, bank(3))
+
+        def cast(copy, grouped, src):
             copy(
                 out=grouped.rearrange("p (c i) t -> p c t i", i=4),
                 in_=src.rearrange("p t (c i) -> p c t i", i=4),
             )
 
-        def quantize(grouped, name):
-            width = grouped.shape[1]
-            codes = keep.tile([P, width], U32, name=name + "_codes", align_bytes=64)
-            scales = keep.tile([P, width], U8, name=name + "_scales", align_bytes=64)
-            nc.vector.quantize_mx(
-                out=codes[:].bitcast(FP8X4), scales=scales[:], in_=grouped.rearrange("p c t -> p (c t)")
-            )
-            return codes, scales
+        def quantize(codes, scales, grouped):
+            nc.vector.quantize_mx(out=codes.bitcast(FP8X4), scales=scales, in_=grouped)
 
-        x_g, x_q = {}, {}
-
-        def cast_x(a):
-            for h in range(2):
-                x_g[a, h] = keep.tile([P, 2 * BLK, PACK], BF16, name="x_g%d%d" % (a, h), align_bytes=64)
-                k0, k1 = ("x", a, 2 * h), ("x", a, 2 * h + 1)
-                if (k0 in ON_VECTOR) == (k1 in ON_VECTOR) and raw[k1][1] == raw[k0][1] + 1:
-                    cast(x_g[a, h][:], k0)
-                else:
-                    cast(x_g[a, h][:, :BLK, :], k0)
-                    cast(x_g[a, h][:, BLK:, :], k1)
-
-        def quantize_x(a):
-            codes = keep.tile([P, J], U32, name="x%d_codes" % a, align_bytes=64)
-            scales = keep.tile([P, J], U8, name="x%d_scales" % a, align_bytes=64)
-            for h in range(2):
-                half = slice(h * J // 2, (h + 1) * J // 2)
-                nc.vector.quantize_mx(
-                    out=codes[:, half].bitcast(FP8X4),
-                    scales=scales[:, half],
-                    in_=x_g[a, h][:].rearrange("p c t -> p (c t)"),
-                )
-            x_q[a] = codes, scales
-
-        u = keep.tile([P, NB, N], F32, name="u")
-
-        def project(g, jb):
-            js = slice(g * J + jb * BLK, g * J + (jb + 1) * BLK)
-            acc = bank(NB * g + jb)
+        def mx(acc, stat, mov, start, stop):
             nc.tensor.matmul_mx(
-                out=acc[:].rearrange("p c n -> p (c n)"),
-                lhsT=got_w[:, js].bitcast(FP8X4),
-                lhsT_scale=got_s[:, js],
-                rhs=w_w[:].bitcast(FP8X4),
-                rhs_scale=w_s[:].bitcast(U8),
-                start=True,
-                stop=True,
-            )
-            return acc[:].rearrange("p c n -> p (c n)")
-
-        def weigh0(jb, acc):
-            t0 = keep.tile([P, N], F32, name="t0_%d" % jb)
-            nc.scalar.activation(out=t0[:], in_=acc, func=ACT.Copy, scale=cols[:, jb : jb + 1])
-            return t0
-
-        def weigh1(jb, acc, t0):
-            nc.vector.scalar_tensor_tensor(
-                out=u[:, jb, :],
-                in0=acc,
-                scalar=cols[:, NB + jb : NB + jb + 1],
-                in1=t0[:],
-                op0=ALU.mult,
-                op1=ALU.add,
+                out=acc,
+                lhsT=stat[0].bitcast(FP8X4),
+                lhsT_scale=stat[1],
+                rhs=mov[0].bitcast(FP8X4),
+                rhs_scale=mov[1],
+                start=start,
+                stop=stop,
             )
 
-        def interpolate():
-            t0 = [weigh0(jb, project(0, jb)) for jb in range(NB)]
+        def turn_add(total, jb, part, start, stop):
+            nc.tensor.matmul(total[:, jb, :], lhsT=part, rhs=ident[:], is_transpose=True, start=start, stop=stop)
+
+        parts = []
+        for g in range(2):
             for jb in range(NB):
-                weigh1(jb, project(1, jb), t0[jb])
-
-        cast_x(0)
-        quantize_x(0)
-        interpolate()
-        cast_x(1)
-        quantize_x(1)
-
-        u_t = []
-        for m in range(NB):
-            turned = bank(m)
-            for jb in range(NB):
-                nc.tensor.transpose(turned[:, jb, :], u[:, jb, m * BLK : (m + 1) * BLK], ident[:])
-            u_m = keep.tile([P, J], F32, name="u_t%d" % m)
-            copy = nc.vector.tensor_copy if m in [] else nc.scalar.copy
-            copy(out=u_m[:], in_=turned[:].rearrange("p c n -> p (c n)"))
-            u_t.append(u_m)
-
-        def front(m):
-            grouped = keep.tile([P, 2 * BLK, PACK], BF16, name="wx_g%d" % m, align_bytes=64)
-            for a in range(2):
-                cast(grouped[:, a * BLK : (a + 1) * BLK, :], ("wx", a, m))
-            wq = [quantize(grouped[:, a * BLK : (a + 1) * BLK, :], "wx%d%d" % (a, m)) for a in range(2)]
-            wq = [(codes[:], scales[:]) for codes, scales in wq]
-            ax_bank = bank(NB + m)
-            ax = ax_bank[:].rearrange("p c n -> p (c n)")
-            for a in range(2):
-                nc.tensor.matmul_mx(
-                    out=ax,
-                    lhsT=wq[a][0].bitcast(FP8X4),
-                    lhsT_scale=wq[a][1],
-                    rhs=x_q[a][0][:].bitcast(FP8X4),
-                    rhs_scale=x_q[a][1][:],
-                    start=(a == 0),
-                    stop=(a == 1),
+                js = slice(g * J + jb * BLK, g * J + (jb + 1) * BLK)
+                acc = bank((NB + jb) if g == 0 else (0, 1, 4, 5)[jb])
+                mx(flat(acc), (got_w[:, js], got_s[:, js]), (w_w[:], w_s[:].bitcast(U8)), True, True)
+                part = keep.tile([P, N], F32, name="part%d%d" % (g, jb))
+                nc.scalar.activation(
+                    out=part[:], in_=flat(acc), func=ACT.Copy, scale=iw_cols[:, g * NB + jb : g * NB + jb + 1]
                 )
-            return ax
+                parts.append((jb, part))
 
-        def back(m, ax):
-            width = J // PIECES[m]
-            for j0 in range(0, J, width):
-                js = slice(j0, j0 + width)
-                s = sums[:, m, :, :].rearrange("p c n -> p (c n)")[:, js]
-                nc.vector.tensor_tensor(out=s, in0=ax[:, js], in1=u_t[m][:, js], op=ALU.add)
-                res = keep.tile([P, width], F32, name="res%d_%d" % (m, j0))
-                nc.scalar.activation(out=res[:], in_=s, func=ACT.Gelu_apprx_tanh, bias=bias[:, m : m + 1])
-                nc.sync.dma_start(out=out[m * BLK : (m + 1) * BLK, js], in_=res[:])
+        to_columns(b_cols, b_rows, bank(6))
 
-        pending = [front(m) for m in range(DEPTH)]
-        sums = keep.tile([P, NB, NB, BLK], F32, name="sums", tag="wx_g1", align_bytes=64)
+        totals = {}
+        for m in reversed(range(NB)):
+            totals[m] = bank((1, 0, 3, 2)[m])
+            for i, (jb, part) in enumerate(parts):
+                last = i == len(parts) - 1 and m >= TURNED
+                turn_add(totals[m], jb, part[:, m * BLK : (m + 1) * BLK], i == 0, last)
+
+        x_q = []
+        for a in range(PASSES):
+            codes = keep.tile([P, J], U32, name="x_codes%d" % a, align_bytes=64)
+            scales = keep.tile([P, J], U8, name="x_scales%d" % a, align_bytes=64)
+            halves = []
+            for h in range(2):
+                grouped = keep.tile([P, HALF, PACK], BF16, name="x_g%d%d" % (a, h), align_bytes=64)
+                cast(nc.vector.tensor_copy, grouped[:], x_raw[a][:, :, h * HALF : (h + 1) * HALF])
+                halves.append(grouped)
+            for h in range(2):
+                hs = slice(h * HALF, (h + 1) * HALF)
+                quantize(codes[:, hs], scales[:, hs], halves[h][:].rearrange("p c t -> p (c t)"))
+            x_q.append((codes, scales))
+
+        def finish(m, src, js, name):
+            res = keep.tile([P, js.stop - js.start], F32, name=name)
+            nc.scalar.activation(
+                out=res[:], in_=src, func=ACT.Gelu_apprx_tanh, bias=b_cols[:, m : m + 1]
+            )
+            nc.sync.dma_start(out=out[m * BLK : (m + 1) * BLK, js], in_=res[:])
+
+        def acc_bank(m):
+            return bank(NB + (m + 2) % NB)
+
+        early, accs = {}, []
         for m in range(NB):
-            back(m, pending[m])
+            grouped = keep.tile([P, PASSES, BLK, PACK], BF16, name="wx_g%d" % m, align_bytes=64)
+            codes = keep.tile([P, PASSES, BLK], U32, name="wx_codes%d" % m, align_bytes=64)
+            scales = keep.tile([P, PASSES, BLK], U8, name="wx_scales%d" % m, align_bytes=64)
+            for a in range(PASSES):
+                cast(nc.vector.tensor_copy, grouped[:, a, :, :], wx_raw[m][a][:])
+            if m == 1:
+                for late in reversed(range(TURNED, NB)):
+                    early[late] = keep.tile([P, J], F32, name="early%d" % late)
+                    nc.scalar.copy(out=early[late][:], in_=flat(totals[late]))
+            if m < NB - 1:
+                quantize(flat(codes), flat(scales), grouped[:].rearrange("p a c t -> p (a c t)"))
+            else:
+                for a in range(PASSES):
+                    quantize(codes[:, a, :], scales[:, a, :], grouped[:, a, :, :].rearrange("p c t -> p (c t)"))
+            wq = [(codes[:, a, :], scales[:, a, :]) for a in range(PASSES)]
+            acc = acc_bank(m)
+            if m < TURNED:
+                for jb in range(NB):
+                    js = slice(jb * BLK, (jb + 1) * BLK)
+                    for a in range(PASSES):
+                        mx(acc[:, jb, :], (x_q[a][0][:, js], x_q[a][1][:, js]), wq[a], a == 0, a == PASSES - 1)
+            else:
+                for a in range(PASSES):
+                    mx(flat(acc), wq[a], (x_q[a][0][:], x_q[a][1][:]), a == 0, a == PASSES - 1)
+            accs.append(acc)
+
+        for m in range(TURNED):
+            dense = keep.tile([P, NB, BLK], F32, name="dense%d" % m)
+            nc.scalar.copy(out=flat(dense), in_=flat(accs[m]))
+            for jb in range(NB):
+                turn_add(totals[m], jb, dense[:, jb, :], False, jb == NB - 1)
+        for m in range(TURNED):
+            finish(m, flat(totals[m]), slice(0, J), "res%d" % m)
+        for m in range(TURNED, NB):
+            pieces = 2 if m == NB - 1 else 1
+            width = J // pieces
+            for i in range(pieces):
+                js = slice(i * width, (i + 1) * width)
+                tag = "wx_g%d" % (NB - 1) if m < NB - 1 else "sum%d" % i
+                total = keep.tile([P, width], F32, name="sum%d%d" % (m, i), tag=tag, align_bytes=64)
+                nc.vector.tensor_tensor(out=total[:], in0=flat(accs[m])[:, js], in1=early[m][:, js], op=ALU.add)
+                finish(m, total[:], js, "res%d%d" % (m, i))

@@ -23,7 +23,6 @@ PASSES = L // K_PASS
 BLK = 128
 NB = 4
 HALF = 256
-TURNED = 2
 
 
 def tile_list_interp_gelu_kernel(
@@ -45,17 +44,15 @@ def tile_list_interp_gelu_kernel(
         tab_s = keep.tile([P, T // 4], I32, name="tab_s", align_bytes=64)
         w_w = keep.tile([P, N], I32, name="w_w", align_bytes=64)
         w_s = keep.tile([P, N // 4], I32, name="w_s", align_bytes=64)
-        iw_rows = keep.tile([P, P], F32, name="iw_rows")
-        b_rows = keep.tile([P, P], F32, name="b_rows")
-        iw_cols = keep.tile([P, 2 * NB], F32, name="iw_cols")
-        b_cols = keep.tile([P, NB], F32, name="b_cols")
+        rows = keep.tile([P, P], F32, name="rows")
+        cols = keep.tile([P, 3 * NB], F32, name="cols")
         ident = keep.tile([P, P], F32, name="ident")
         warm = keep.tile([P, 8], F32, name="warm")
 
         nc.vector.memset(tab_s[:], 0)
-        nc.vector.memset(iw_rows[:], 0.0)
+        nc.vector.memset(rows[:], 0.0)
         nc.vector.memset(w_s[:], 0)
-        nc.vector.memset(b_rows[:], 0.0)
+        nc.vector.memset(warm[:, 4:8], 0.0)
         make_identity(nc, ident[:])
 
         def load_words(dst, src):
@@ -64,11 +61,11 @@ def tile_list_interp_gelu_kernel(
         def load_scales(queue, dst, src, r):
             queue.dma_start(out=dst[r:P:32, :], in_=src[0].bitcast(I32)[r:16:4, :])
 
-        def load_vector(queue, rows, i, vec):
+        def load_vector(queue, i, vec):
             queue.dma_start(out=rows[i * NB : (i + 1) * NB, :], in_=vec.rearrange("(c p) -> c p", p=P))
 
         def load_rows(src, a, first, width, name):
-            chunk = keep.tile([P, PACK, width], F32, name=name)
+            chunk = keep.tile([P, PACK, width], F32, name=name, align_bytes=64)
             nc.sync.dma_start(
                 out=chunk[:],
                 in_=src[a * K_PASS : (a + 1) * K_PASS, first : first + width].rearrange("(p t) c -> p t c", t=PACK),
@@ -79,15 +76,14 @@ def tile_list_interp_gelu_kernel(
         load_words(w_w, w_words)
         for r in range(4):
             load_scales(nc.sync if r < 3 else nc.scalar, tab_s, tab_scales, r)
-        nc.scalar.activation(out=warm[:, 0:1], in_=b_rows[:, 0:1], func=ACT.Gelu_apprx_tanh)
+        load_vector(nc.scalar, 2, b)
+        nc.scalar.activation(out=warm[:, 0:1], in_=warm[:, 4:5], func=ACT.Gelu_apprx_tanh)
         load_words(tab_w, tab_words)
-        load_vector(nc.sync, iw_rows, 0, iw0)
-        load_vector(nc.sync, iw_rows, 1, iw1)
+        load_vector(nc.sync, 0, iw0)
+        load_vector(nc.sync, 1, iw1)
         for r in range(4):
             load_scales(nc.sync, w_s, w_scales, r)
-        x_raw = [load_rows(x, 0, 0, J, "x_raw0")]
-        load_vector(nc.sync, b_rows, 0, b)
-        x_raw.append(load_rows(x, 1, 0, J, "x_raw1"))
+        x_raw = [load_rows(x, a, 0, J, "x_raw%d" % a) for a in range(PASSES)]
         wx_raw = [[load_rows(wx, a, m * BLK, BLK, "wx_raw%d%d" % (m, a)) for a in range(PASSES)] for m in range(NB)]
 
         got_s = keep.tile([P, 2 * J], U8, name="got_s", align_bytes=64)
@@ -99,11 +95,9 @@ def tile_list_interp_gelu_kernel(
                 tab_w[:].bitcast(U32).indirect(offsets[:, i * HALF // 16 : (i + 1) * HALF // 16]),
             )
 
-        def to_columns(cols, rows, turned):
-            nc.tensor.transpose(turned[:, 0, :], rows[:], ident[:])
-            nc.scalar.copy(out=cols[:], in_=turned[:, 0, 0 : cols.shape[1]])
-
-        to_columns(iw_cols, iw_rows, bank(3))
+        turned = bank(NB - 1)
+        nc.tensor.transpose(turned[:, 0, :], rows[:], ident[:])
+        nc.scalar.copy(out=cols[:], in_=turned[:, 0, 0 : 3 * NB])
 
         def cast(copy, grouped, src):
             copy(
@@ -132,22 +126,19 @@ def tile_list_interp_gelu_kernel(
         for g in range(2):
             for jb in range(NB):
                 js = slice(g * J + jb * BLK, g * J + (jb + 1) * BLK)
-                acc = bank((NB + jb) if g == 0 else (0, 1, 4, 5)[jb])
+                acc = bank(NB + jb)
                 mx(flat(acc), (got_w[:, js], got_s[:, js]), (w_w[:], w_s[:].bitcast(U8)), True, True)
                 part = keep.tile([P, N], F32, name="part%d%d" % (g, jb))
                 nc.scalar.activation(
-                    out=part[:], in_=flat(acc), func=ACT.Copy, scale=iw_cols[:, g * NB + jb : g * NB + jb + 1]
+                    out=part[:], in_=flat(acc), func=ACT.Copy, scale=cols[:, g * NB + jb : g * NB + jb + 1]
                 )
                 parts.append((jb, part))
 
-        to_columns(b_cols, b_rows, bank(6))
 
-        totals = {}
-        for m in reversed(range(NB)):
-            totals[m] = bank((1, 0, 3, 2)[m])
-            for i, (jb, part) in enumerate(parts):
-                last = i == len(parts) - 1 and m >= TURNED
-                turn_add(totals[m], jb, part[:, m * BLK : (m + 1) * BLK], i == 0, last)
+        totals = [bank(m) for m in range(NB)]
+        for i, (jb, part) in enumerate(parts):
+            for m in range(NB):
+                turn_add(totals[m], jb, part[:, m * BLK : (m + 1) * BLK], i == 0, i == len(parts) - 1)
 
         x_q = []
         for a in range(PASSES):
@@ -163,57 +154,46 @@ def tile_list_interp_gelu_kernel(
                 quantize(codes[:, hs], scales[:, hs], halves[h][:].rearrange("p c t -> p (c t)"))
             x_q.append((codes, scales))
 
-        def finish(m, src, js, name):
-            res = keep.tile([P, js.stop - js.start], F32, name=name)
+        def finish(m, src, js, name, tag):
+            res = keep.tile([P, js.stop - js.start], F32, name=name, tag=tag, align_bytes=64)
             nc.scalar.activation(
-                out=res[:], in_=src, func=ACT.Gelu_apprx_tanh, bias=b_cols[:, m : m + 1]
+                out=res[:], in_=src, func=ACT.Gelu_apprx_tanh, bias=cols[:, 2 * NB + m : 2 * NB + m + 1]
             )
             nc.sync.dma_start(out=out[m * BLK : (m + 1) * BLK, js], in_=res[:])
 
         def acc_bank(m):
-            return bank(NB + (m + 2) % NB)
+            return bank(NB + m)
+        last = NB - 1
 
-        early, accs = {}, []
-        for m in range(NB):
+        def dense_product(m):
             grouped = keep.tile([P, PASSES, BLK, PACK], BF16, name="wx_g%d" % m, align_bytes=64)
             codes = keep.tile([P, PASSES, BLK], U32, name="wx_codes%d" % m, align_bytes=64)
             scales = keep.tile([P, PASSES, BLK], U8, name="wx_scales%d" % m, align_bytes=64)
             for a in range(PASSES):
-                cast(nc.vector.tensor_copy, grouped[:, a, :, :], wx_raw[m][a][:])
-            if m == 1:
-                for late in reversed(range(TURNED, NB)):
-                    early[late] = keep.tile([P, J], F32, name="early%d" % late)
-                    nc.scalar.copy(out=early[late][:], in_=flat(totals[late]))
-            if m < NB - 1:
+                cast(nc.scalar.copy if (m, a) == (1, 0) else nc.vector.tensor_copy, grouped[:, a, :, :], wx_raw[m][a][:])
+            if m < last:
                 quantize(flat(codes), flat(scales), grouped[:].rearrange("p a c t -> p (a c t)"))
             else:
                 for a in range(PASSES):
                     quantize(codes[:, a, :], scales[:, a, :], grouped[:, a, :, :].rearrange("p c t -> p (c t)"))
-            wq = [(codes[:, a, :], scales[:, a, :]) for a in range(PASSES)]
             acc = acc_bank(m)
-            if m < TURNED:
-                for jb in range(NB):
-                    js = slice(jb * BLK, (jb + 1) * BLK)
-                    for a in range(PASSES):
-                        mx(acc[:, jb, :], (x_q[a][0][:, js], x_q[a][1][:, js]), wq[a], a == 0, a == PASSES - 1)
-            else:
-                for a in range(PASSES):
-                    mx(flat(acc), wq[a], (x_q[a][0][:], x_q[a][1][:]), a == 0, a == PASSES - 1)
-            accs.append(acc)
+            for a in range(PASSES):
+                mx(flat(acc), (codes[:, a, :], scales[:, a, :]), (x_q[a][0][:], x_q[a][1][:]), a == 0, a == PASSES - 1)
+            return acc
 
-        for m in range(TURNED):
-            dense = keep.tile([P, NB, BLK], F32, name="dense%d" % m)
-            nc.scalar.copy(out=flat(dense), in_=flat(accs[m]))
-            for jb in range(NB):
-                turn_add(totals[m], jb, dense[:, jb, :], False, jb == NB - 1)
-        for m in range(TURNED):
-            finish(m, flat(totals[m]), slice(0, J), "res%d" % m)
-        for m in range(TURNED, NB):
-            pieces = 2 if m == NB - 1 else 1
+        accs = [dense_product(m) for m in range(NB)]
+
+        early = keep.tile([P, NB, J], F32, name="early", tag="wx_raw10", align_bytes=64)
+        for m in range(NB):
+            nc.scalar.copy(out=early[:, m, :], in_=flat(totals[m]))
+
+        slots = ["wx_raw21", "wx_raw31", "wx_g3"]
+        for m in range(NB):
+            pieces = 2 if m == last else 1
             width = J // pieces
             for i in range(pieces):
                 js = slice(i * width, (i + 1) * width)
-                tag = "wx_g%d" % (NB - 1) if m < NB - 1 else "sum%d" % i
+                tag = slots[m] if m < last else "sum%d" % i
                 total = keep.tile([P, width], F32, name="sum%d%d" % (m, i), tag=tag, align_bytes=64)
-                nc.vector.tensor_tensor(out=total[:], in0=flat(accs[m])[:, js], in1=early[m][:, js], op=ALU.add)
-                finish(m, total[:], js, "res%d%d" % (m, i))
+                nc.vector.tensor_tensor(out=total[:], in0=flat(accs[m])[:, js], in1=early[:, m, js], op=ALU.add)
+                finish(m, total[:], js, "res%d%d" % (m, i), "res%d%d" % (m, i))

@@ -84,7 +84,7 @@ def tile_list_interp_gelu_kernel(
         for r in range(4):
             load_scales(nc.sync, w_s, w_scales, r)
         x_raw = [load_rows(x, a, 0, J, "x_raw%d" % a) for a in range(PASSES)]
-        wx_raw = [[load_rows(wx, a, m * BLK, BLK, "wx_raw%d%d" % (m, a)) for a in range(PASSES)] for m in range(NB)]
+        wx_raw = [[load_rows(wx, a, h * HALF, HALF, "wx_raw%d%d" % (h, a)) for a in range(PASSES)] for h in range(2)]
 
         got_s = keep.tile([P, 2 * J], U8, name="got_s", align_bytes=64)
         got_w = keep.tile([P, 2 * J], U32, name="got_w", align_bytes=64)
@@ -165,29 +165,31 @@ def tile_list_interp_gelu_kernel(
             return bank(NB + m)
         last = NB - 1
 
-        def dense_product(m):
-            grouped = keep.tile([P, PASSES, BLK, PACK], BF16, name="wx_g%d" % m, align_bytes=64)
-            codes = keep.tile([P, PASSES, BLK], U32, name="wx_codes%d" % m, align_bytes=64)
-            scales = keep.tile([P, PASSES, BLK], U8, name="wx_scales%d" % m, align_bytes=64)
+        def dense_products(h):
+            blocks = (2 * h, 2 * h + 1)
+            grouped = [keep.tile([P, PASSES, BLK, PACK], BF16, name="wx_g%d" % m, align_bytes=64) for m in blocks]
             for a in range(PASSES):
-                cast(nc.scalar.copy if (m, a) == (1, 0) else nc.vector.tensor_copy, grouped[:, a, :, :], wx_raw[m][a][:])
-            if m < last:
-                quantize(flat(codes), flat(scales), grouped[:].rearrange("p a c t -> p (a c t)"))
-            else:
+                for i in range(2):
+                    copy = nc.scalar.copy if (h, a, i) == (0, 0, 1) else nc.vector.tensor_copy
+                    cast(copy, grouped[i][:, a, :, :], wx_raw[h][a][:, :, i * BLK : (i + 1) * BLK])
+            found = []
+            for i, m in enumerate(blocks):
+                codes = keep.tile([P, PASSES, BLK], U32, name="wx_codes%d" % m, align_bytes=64)
+                scales = keep.tile([P, PASSES, BLK], U8, name="wx_scales%d" % m, align_bytes=64)
+                quantize(flat(codes), flat(scales), grouped[i][:].rearrange("p a c t -> p (a c t)"))
+                acc = acc_bank(m)
                 for a in range(PASSES):
-                    quantize(codes[:, a, :], scales[:, a, :], grouped[:, a, :, :].rearrange("p c t -> p (c t)"))
-            acc = acc_bank(m)
-            for a in range(PASSES):
-                mx(flat(acc), (codes[:, a, :], scales[:, a, :]), (x_q[a][0][:], x_q[a][1][:]), a == 0, a == PASSES - 1)
-            return acc
+                    mx(flat(acc), (codes[:, a, :], scales[:, a, :]), (x_q[a][0][:], x_q[a][1][:]), a == 0, a == PASSES - 1)
+                found.append(acc)
+            return found
 
-        accs = [dense_product(m) for m in range(NB)]
+        accs = dense_products(0) + dense_products(1)
 
-        early = keep.tile([P, NB, J], F32, name="early", tag="wx_raw10", align_bytes=64)
+        early = keep.tile([P, NB, J], F32, name="early", tag="wx_raw00", align_bytes=64)
         for m in range(NB):
             nc.scalar.copy(out=early[:, m, :], in_=flat(totals[m]))
 
-        slots = ["wx_raw21", "wx_raw31", "wx_g3"]
+        slots = ["wx_raw10", "wx_g3", "wx_g2"]
         for m in range(NB):
             pieces = 2 if m == last else 1
             width = J // pieces

@@ -84,7 +84,10 @@ def tile_list_interp_gelu_kernel(
         for r in range(4):
             load_scales(nc.sync, w_s, w_scales, r)
         x_raw = [load_rows(x, a, 0, J, "x_raw%d" % a) for a in range(PASSES)]
-        wx_raw = [[load_rows(wx, a, h * HALF, HALF, "wx_raw%d%d" % (h, a)) for a in range(PASSES)] for h in range(2)]
+        wx_pair = [load_rows(wx, a, 0, HALF, "wx_pair%d" % a) for a in range(PASSES)]
+        wx_raw = [[wx_pair[a][:, :, m * BLK : (m + 1) * BLK] for a in range(PASSES)] for m in range(2)]
+        for m in range(2, NB):
+            wx_raw.append([load_rows(wx, a, m * BLK, BLK, "wx_raw%d%d" % (m, a))[:] for a in range(PASSES)])
 
         got_s = keep.tile([P, 2 * J], U8, name="got_s", align_bytes=64)
         got_w = keep.tile([P, 2 * J], U32, name="got_w", align_bytes=64)
@@ -164,38 +167,43 @@ def tile_list_interp_gelu_kernel(
         def acc_bank(m):
             return bank(NB + m)
         last = NB - 1
+        grouped = [keep.tile([P, PASSES, BLK, PACK], BF16, name="wx_g%d" % m, align_bytes=64) for m in range(NB)]
+        accs = [acc_bank(m) for m in range(NB)]
+        on_scalar = ((1, 0), (2, 1))
 
-        def dense_products(h):
-            blocks = (2 * h, 2 * h + 1)
-            grouped = [keep.tile([P, PASSES, BLK, PACK], BF16, name="wx_g%d" % m, align_bytes=64) for m in blocks]
+        def cast_wx(m, a):
+            cast(nc.scalar.copy if (m, a) in on_scalar else nc.vector.tensor_copy, grouped[m][:, a, :, :], wx_raw[m][a])
+
+        def multiply(m):
+            codes = keep.tile([P, PASSES, BLK], U32, name="wx_codes%d" % m, align_bytes=64)
+            scales = keep.tile([P, PASSES, BLK], U8, name="wx_scales%d" % m, align_bytes=64)
+            quantize(flat(codes), flat(scales), grouped[m][:].rearrange("p a c t -> p (a c t)"))
             for a in range(PASSES):
-                for i in range(2):
-                    copy = nc.scalar.copy if (h, a, i) == (0, 0, 1) else nc.vector.tensor_copy
-                    cast(copy, grouped[i][:, a, :, :], wx_raw[h][a][:, :, i * BLK : (i + 1) * BLK])
-            found = []
-            for i, m in enumerate(blocks):
-                codes = keep.tile([P, PASSES, BLK], U32, name="wx_codes%d" % m, align_bytes=64)
-                scales = keep.tile([P, PASSES, BLK], U8, name="wx_scales%d" % m, align_bytes=64)
-                quantize(flat(codes), flat(scales), grouped[i][:].rearrange("p a c t -> p (a c t)"))
-                acc = acc_bank(m)
-                for a in range(PASSES):
-                    mx(flat(acc), (codes[:, a, :], scales[:, a, :]), (x_q[a][0][:], x_q[a][1][:]), a == 0, a == PASSES - 1)
-                found.append(acc)
-            return found
+                mx(flat(accs[m]), (codes[:, a, :], scales[:, a, :]), (x_q[a][0][:], x_q[a][1][:]), a == 0, a == PASSES - 1)
 
-        accs = dense_products(0) + dense_products(1)
+        for a in range(PASSES):
+            for m in range(2):
+                cast_wx(m, a)
+        for m in range(2):
+            multiply(m)
+        for m in range(2, NB):
+            for a in range(PASSES):
+                cast_wx(m, a)
+        multiply(2)
 
-        early = keep.tile([P, NB, J], F32, name="early", tag="wx_raw00", align_bytes=64)
+        early = keep.tile([P, NB, J], F32, name="early", tag="wx_raw21", align_bytes=64)
         for m in range(NB):
             nc.scalar.copy(out=early[:, m, :], in_=flat(totals[m]))
 
-        slots = ["wx_raw10", "wx_g3", "wx_g2"]
-        for m in range(NB):
-            pieces = 2 if m == last else 1
-            width = J // pieces
-            for i in range(pieces):
-                js = slice(i * width, (i + 1) * width)
-                tag = slots[m] if m < last else "sum%d" % i
-                total = keep.tile([P, width], F32, name="sum%d%d" % (m, i), tag=tag, align_bytes=64)
-                nc.vector.tensor_tensor(out=total[:], in0=flat(accs[m])[:, js], in1=early[:, m, js], op=ALU.add)
-                finish(m, total[:], js, "res%d%d" % (m, i), "res%d%d" % (m, i))
+        def add_early(m, j0, j1):
+            js = slice(j0, j1)
+            total = keep.tile([P, j1 - j0], F32, name="sum%d_%d" % (m, j0))
+            nc.vector.tensor_tensor(out=total[:], in0=flat(accs[m])[:, js], in1=early[:, m, js], op=ALU.add)
+            finish(m, total[:], js, "res%d_%d" % (m, j0), "res%d_%d" % (m, j0))
+
+        add_early(0, 0, J)
+        multiply(last)
+        for m in range(1, last):
+            add_early(m, 0, J)
+        add_early(last, 0, J - BLK)
+        add_early(last, J - BLK, J)

@@ -126,22 +126,25 @@ def tile_list_interp_gelu_kernel(
             nc.tensor.matmul(total[:, jb, :], lhsT=part, rhs=ident[:], is_transpose=True, start=start, stop=stop)
 
         parts = []
+        weighted = [keep.tile([P, NB, N], F32, name="weighted%d" % g) for g in range(2)]
         for g in range(2):
             for jb in range(NB):
                 js = slice(g * J + jb * BLK, g * J + (jb + 1) * BLK)
                 acc = bank(NB + jb)
                 mx(flat(acc), (got_w[:, js], got_s[:, js]), (w_w[:], w_s[:].bitcast(U8)), True, True)
-                part = keep.tile([P, N], F32, name="part%d%d" % (g, jb))
+                part = weighted[g][:, jb, :]
                 nc.scalar.activation(
-                    out=part[:], in_=flat(acc), func=ACT.Copy, scale=cols[:, g * NB + jb : g * NB + jb + 1]
+                    out=part, in_=flat(acc), func=ACT.Copy, scale=cols[:, g * NB + jb : g * NB + jb + 1]
                 )
                 parts.append((jb, part))
 
 
         totals = [bank(m) for m in range(NB)]
         for i, (jb, part) in enumerate(parts):
-            for m in range(NB):
+            for m in range(1, NB):
                 turn_add(totals[m], jb, part[:, m * BLK : (m + 1) * BLK], i == 0, i == len(parts) - 1)
+            if i >= NB:
+                turn_add(totals[0], jb, part[:, :BLK], i == NB, False)
 
         x_q = []
         for a in range(PASSES):
@@ -169,31 +172,44 @@ def tile_list_interp_gelu_kernel(
         last = NB - 1
         grouped = [keep.tile([P, PASSES, BLK, PACK], BF16, name="wx_g%d" % m, align_bytes=64) for m in range(NB)]
         accs = [acc_bank(m) for m in range(NB)]
-        on_scalar = ((1, 0), (2, 1))
+        on_scalar = ((1, 0), (3, 0))
 
         def cast_wx(m, a):
             cast(nc.scalar.copy if (m, a) in on_scalar else nc.vector.tensor_copy, grouped[m][:, a, :, :], wx_raw[m][a])
 
-        def multiply(m):
-            codes = keep.tile([P, PASSES, BLK], U32, name="wx_codes%d" % m, align_bytes=64)
-            scales = keep.tile([P, PASSES, BLK], U8, name="wx_scales%d" % m, align_bytes=64)
-            quantize(flat(codes), flat(scales), grouped[m][:].rearrange("p a c t -> p (a c t)"))
-            for a in range(PASSES):
-                mx(flat(accs[m]), (codes[:, a, :], scales[:, a, :]), (x_q[a][0][:], x_q[a][1][:]), a == 0, a == PASSES - 1)
+        def multiply(m, passes=range(PASSES)):
+            name = "wx%d%d" % (m, passes.start)
+            codes = keep.tile([P, len(passes), BLK], U32, name=name + "_codes", align_bytes=64)
+            scales = keep.tile([P, len(passes), BLK], U8, name=name + "_scales", align_bytes=64)
+            source = grouped[m][:, passes.start : passes.stop, :, :]
+            quantize(flat(codes), flat(scales), source.rearrange("p a c t -> p (a c t)"))
+            wq = {a: (codes[:, i, :], scales[:, i, :]) for i, a in enumerate(passes)}
+            for jb in range(NB if m == 0 else 0):
+                js = slice(jb * BLK, (jb + 1) * BLK)
+                for a in range(PASSES):
+                    mx(accs[m][:, jb, :], (x_q[a][0][:, js], x_q[a][1][:, js]), wq[a], a == 0, a == PASSES - 1)
+            for a in passes if m > 0 else []:
+                mx(flat(accs[m]), wq[a], (x_q[a][0][:], x_q[a][1][:]), a == 0, a == PASSES - 1)
 
         for a in range(PASSES):
             for m in range(2):
                 cast_wx(m, a)
         for m in range(2):
             multiply(m)
-        for m in range(2, NB):
-            for a in range(PASSES):
-                cast_wx(m, a)
-        multiply(2)
+        for a in range(PASSES):
+            cast_wx(2, a)
 
-        early = keep.tile([P, NB, J], F32, name="early", tag="wx_raw21", align_bytes=64)
-        for m in range(NB):
+        first_sum = keep.tile([P, NB, BLK], F32, name="first_sum")
+        nc.vector.tensor_tensor(out=first_sum[:], in0=accs[0][:], in1=weighted[0][:, :, :BLK], op=ALU.add)
+        for jb in range(NB):
+            turn_add(totals[0], jb, first_sum[:, jb, :], False, jb == NB - 1)
+
+        multiply(2)
+        early = keep.tile([P, NB, J], F32, name="early", tag="wx_pair0", align_bytes=64)
+        for m in range(1, NB):
             nc.scalar.copy(out=early[:, m, :], in_=flat(totals[m]))
+        for a in range(PASSES):
+            cast_wx(last, a)
 
         def add_early(m, j0, j1):
             js = slice(j0, j1)
@@ -201,9 +217,10 @@ def tile_list_interp_gelu_kernel(
             nc.vector.tensor_tensor(out=total[:], in0=flat(accs[m])[:, js], in1=early[:, m, js], op=ALU.add)
             finish(m, total[:], js, "res%d_%d" % (m, j0), "res%d_%d" % (m, j0))
 
-        add_early(0, 0, J)
-        multiply(last)
-        for m in range(1, last):
-            add_early(m, 0, J)
+        add_early(1, 0, J)
+        finish(0, flat(totals[0]), slice(0, J), "res0", "res0")
+        multiply(last, range(0, 1))
+        multiply(last, range(1, 2))
+        add_early(2, 0, J)
         add_early(last, 0, J - BLK)
         add_early(last, J - BLK, J)

@@ -23,6 +23,7 @@ PASSES = L // K_PASS
 BLK = 128
 NB = 4
 HALF = 256
+TURNED = 1
 
 
 def tile_list_interp_gelu_kernel(
@@ -83,8 +84,10 @@ def tile_list_interp_gelu_kernel(
         load_vector(nc.sync, 1, iw1)
         for r in range(4):
             load_scales(nc.sync, w_s, w_scales, r)
-        x_raw = [load_rows(x, a, 0, J, "x_raw%d" % a) for a in range(PASSES)]
-        wx_pair = [load_rows(wx, a, 0, HALF, "wx_pair%d" % a) for a in range(PASSES)]
+        x_raw, wx_pair = [], []
+        for a in range(PASSES):
+            x_raw.append(load_rows(x, a, 0, J, "x_raw%d" % a))
+            wx_pair.append(load_rows(wx, a, 0, HALF, "wx_pair%d" % a))
         wx_raw = [[wx_pair[a][:, :, m * BLK : (m + 1) * BLK] for a in range(PASSES)] for m in range(2)]
         for m in range(2, NB):
             wx_raw.append([load_rows(wx, a, m * BLK, BLK, "wx_raw%d%d" % (m, a))[:] for a in range(PASSES)])
@@ -139,22 +142,15 @@ def tile_list_interp_gelu_kernel(
                 parts.append((jb, part))
 
 
-        totals = [bank(m) for m in range(NB)]
-        for i, (jb, part) in enumerate(parts):
-            for m in range(1, NB):
-                turn_add(totals[m], jb, part[:, m * BLK : (m + 1) * BLK], i == 0, i == len(parts) - 1)
-            if i >= NB:
-                turn_add(totals[0], jb, part[:, :BLK], i == NB, False)
-
         x_q = []
-        for a in range(PASSES):
+
+        def quantize_x(a):
             codes = keep.tile([P, J], U32, name="x_codes%d" % a, align_bytes=64)
             scales = keep.tile([P, J], U8, name="x_scales%d" % a, align_bytes=64)
             halves = []
             for h in range(2):
-                grouped = keep.tile([P, HALF, PACK], BF16, name="x_g%d%d" % (a, h), align_bytes=64)
-                cast(nc.vector.tensor_copy, grouped[:], x_raw[a][:, :, h * HALF : (h + 1) * HALF])
-                halves.append(grouped)
+                halves.append(keep.tile([P, HALF, PACK], BF16, name="x_g%d%d" % (a, h), align_bytes=64))
+                cast(nc.vector.tensor_copy, halves[h][:], x_raw[a][:, :, h * HALF : (h + 1) * HALF])
             for h in range(2):
                 hs = slice(h * HALF, (h + 1) * HALF)
                 quantize(codes[:, hs], scales[:, hs], halves[h][:].rearrange("p c t -> p (c t)"))
@@ -172,7 +168,7 @@ def tile_list_interp_gelu_kernel(
         last = NB - 1
         grouped = [keep.tile([P, PASSES, BLK, PACK], BF16, name="wx_g%d" % m, align_bytes=64) for m in range(NB)]
         accs = [acc_bank(m) for m in range(NB)]
-        on_scalar = ((1, 0), (3, 0))
+        on_scalar = ((1, 1), (3, 0))
 
         def cast_wx(m, a):
             cast(nc.scalar.copy if (m, a) in on_scalar else nc.vector.tensor_copy, grouped[m][:, a, :, :], wx_raw[m][a])
@@ -184,29 +180,44 @@ def tile_list_interp_gelu_kernel(
             source = grouped[m][:, passes.start : passes.stop, :, :]
             quantize(flat(codes), flat(scales), source.rearrange("p a c t -> p (a c t)"))
             wq = {a: (codes[:, i, :], scales[:, i, :]) for i, a in enumerate(passes)}
-            for jb in range(NB if m == 0 else 0):
+            for jb in range(NB if m < TURNED else 0):
                 js = slice(jb * BLK, (jb + 1) * BLK)
-                for a in range(PASSES):
-                    mx(accs[m][:, jb, :], (x_q[a][0][:, js], x_q[a][1][:, js]), wq[a], a == 0, a == PASSES - 1)
-            for a in passes if m > 0 else []:
+                for a in passes:
+                    first, final = (a, jb) == (0, 0), (a, jb) == (PASSES - 1, NB - 1)
+                    mx(accs[m][:, jb, :], (x_q[a][0][:, js], x_q[a][1][:, js]), wq[a], first, final)
+            for a in passes if m >= TURNED else []:
                 mx(flat(accs[m]), wq[a], (x_q[a][0][:], x_q[a][1][:]), a == 0, a == PASSES - 1)
 
-        for a in range(PASSES):
+        def first_pair(a):
+            quantize_x(a)
             for m in range(2):
                 cast_wx(m, a)
-        for m in range(2):
-            multiply(m)
+            for m in range(2):
+                multiply(m, range(a, a + 1))
+
+        first_pair(0)
+        totals = [bank(m) for m in range(NB)]
+        for i, (jb, part) in enumerate(parts):
+            for m in range(TURNED, NB):
+                turn_add(totals[m], jb, part[:, m * BLK : (m + 1) * BLK], i == 0, i == len(parts) - 1)
+            for m in range(TURNED if i >= NB else 0):
+                turn_add(totals[m], jb, part[:, m * BLK : (m + 1) * BLK], i == NB, False)
+
+        first_pair(1)
         for a in range(PASSES):
             cast_wx(2, a)
 
-        first_sum = keep.tile([P, NB, BLK], F32, name="first_sum")
-        nc.vector.tensor_tensor(out=first_sum[:], in0=accs[0][:], in1=weighted[0][:, :, :BLK], op=ALU.add)
-        for jb in range(NB):
-            turn_add(totals[0], jb, first_sum[:, jb, :], False, jb == NB - 1)
+        def add_turned(m):
+            total = keep.tile([P, NB, BLK], F32, name="turned_sum%d" % m)
+            block = weighted[0][:, :, m * BLK : (m + 1) * BLK]
+            nc.vector.tensor_tensor(out=total[:], in0=accs[m][:], in1=block, op=ALU.add)
+            for jb in range(NB):
+                turn_add(totals[m], jb, total[:, jb, :], False, jb == NB - 1)
 
+        add_turned(0)
         multiply(2)
-        early = keep.tile([P, NB, J], F32, name="early", tag="wx_pair0", align_bytes=64)
-        for m in range(1, NB):
+        early = keep.tile([P, NB, J], F32, name="early", tag="wx_pair1", align_bytes=64)
+        for m in range(TURNED, NB):
             nc.scalar.copy(out=early[:, m, :], in_=flat(totals[m]))
         for a in range(PASSES):
             cast_wx(last, a)

@@ -164,7 +164,7 @@ def tile_list_interp_gelu_kernel(
             nc.sync.dma_start(out=out[m * BLK : (m + 1) * BLK, js], in_=res[:])
 
         def acc_bank(m):
-            return bank(NB + m)
+            return bank(NB + m if m < NB - 1 else 0)
         last = NB - 1
         grouped = [keep.tile([P, PASSES, BLK, PACK], BF16, name="wx_g%d" % m, align_bytes=64) for m in range(NB)]
         accs = [acc_bank(m) for m in range(NB)]
@@ -196,14 +196,14 @@ def tile_list_interp_gelu_kernel(
                 multiply(m, range(a, a + 1))
 
         first_pair(0)
-        totals = [bank(m) for m in range(NB)]
+        totals = [bank(m if m > 0 else 2 * NB - 1) for m in range(NB)]
         for i, (jb, part) in enumerate(parts):
             for m in range(TURNED, NB):
                 turn_add(totals[m], jb, part[:, m * BLK : (m + 1) * BLK], i == 0, i == len(parts) - 1)
-            for m in range(TURNED if i >= NB else 0):
-                turn_add(totals[m], jb, part[:, m * BLK : (m + 1) * BLK], i == NB, False)
 
         first_pair(1)
+        for jb, part in parts[NB:]:
+            turn_add(totals[0], jb, part[:, :BLK], jb == 0, False)
         for a in range(PASSES):
             cast_wx(2, a)
 
@@ -232,6 +232,8 @@ def tile_list_interp_gelu_kernel(
         finish(0, flat(totals[0]), slice(0, J), "res0", "res0")
         multiply(last, range(0, 1))
         multiply(last, range(1, 2))
-        add_early(2, 0, J)
-        add_early(last, 0, J - BLK)
+        add_early(2, 0, HALF)
+        add_early(2, HALF, J)
+        add_early(last, 0, HALF)
+        add_early(last, HALF, J - BLK)
         add_early(last, J - BLK, J)

@@ -135,11 +135,26 @@ def tile_list_interp_gelu_kernel(
                 js = slice(g * J + jb * BLK, g * J + (jb + 1) * BLK)
                 acc = bank(NB + jb)
                 mx(flat(acc), (got_w[:, js], got_s[:, js]), (w_w[:], w_s[:].bitcast(U8)), True, True)
+                if (g, jb) == (1, 0):
+                    held = acc
+                    continue
                 part = weighted[g][:, jb, :]
                 nc.scalar.activation(
                     out=part, in_=flat(acc), func=ACT.Copy, scale=cols[:, g * NB + jb : g * NB + jb + 1]
                 )
                 parts.append((jb, part))
+
+        def combine():
+            both = keep.tile([P, N], F32, name="both", tag="wx_pair0", align_bytes=64)
+            nc.vector.scalar_tensor_tensor(
+                out=both[:],
+                in0=flat(held),
+                scalar=cols[:, NB : NB + 1],
+                in1=parts[0][1],
+                op0=ALU.mult,
+                op1=ALU.add,
+            )
+            return both
 
 
         x_q = []
@@ -150,7 +165,7 @@ def tile_list_interp_gelu_kernel(
             halves = []
             for h in range(2):
                 halves.append(keep.tile([P, HALF, PACK], BF16, name="x_g%d%d" % (a, h), align_bytes=64))
-                cast(nc.vector.tensor_copy, halves[h][:], x_raw[a][:, :, h * HALF : (h + 1) * HALF])
+                cast(nc.scalar.copy if (a, h) == (1, 1) else nc.vector.tensor_copy, halves[h][:], x_raw[a][:, :, h * HALF : (h + 1) * HALF])
             for h in range(2):
                 hs = slice(h * HALF, (h + 1) * HALF)
                 quantize(codes[:, hs], scales[:, hs], halves[h][:].rearrange("p c t -> p (c t)"))
@@ -164,10 +179,10 @@ def tile_list_interp_gelu_kernel(
             nc.sync.dma_start(out=out[m * BLK : (m + 1) * BLK, js], in_=res[:])
 
         def acc_bank(m):
-            return bank(NB + m if m < NB - 1 else 0)
+            return bank((5, 6, 4, 0)[m])
         last = NB - 1
         grouped = [keep.tile([P, PASSES, BLK, PACK], BF16, name="wx_g%d" % m, align_bytes=64) for m in range(NB)]
-        accs = [acc_bank(m) for m in range(NB)]
+        accs = {m: acc_bank(m) for m in (0, 1, 3)}
         on_scalar = ((1, 1), (3, 0))
 
         def cast_wx(m, a):
@@ -196,21 +211,27 @@ def tile_list_interp_gelu_kernel(
                 multiply(m, range(a, a + 1))
 
         first_pair(0)
+        both = combine()
+        accs[2] = acc_bank(2)
+        late = parts[NB:]
+        parts = parts[1:NB] + late[:2] + [(0, both[:])] + late[2:]
         totals = [bank(m if m > 0 else 2 * NB - 1) for m in range(NB)]
         for i, (jb, part) in enumerate(parts):
             for m in range(TURNED, NB):
                 turn_add(totals[m], jb, part[:, m * BLK : (m + 1) * BLK], i == 0, i == len(parts) - 1)
 
         first_pair(1)
-        for jb, part in parts[NB:]:
-            turn_add(totals[0], jb, part[:, :BLK], jb == 0, False)
+        for jb, part in late:
+            turn_add(totals[0], jb, part[:, :BLK], jb == 1, False)
         for a in range(PASSES):
             cast_wx(2, a)
 
         def add_turned(m):
             total = keep.tile([P, NB, BLK], F32, name="turned_sum%d" % m)
             block = weighted[0][:, :, m * BLK : (m + 1) * BLK]
-            nc.vector.tensor_tensor(out=total[:], in0=accs[m][:], in1=block, op=ALU.add)
+            first = both[:, m * BLK : (m + 1) * BLK]
+            nc.vector.tensor_tensor(out=total[:, 0, :], in0=accs[m][:, 0, :], in1=first, op=ALU.add)
+            nc.vector.tensor_tensor(out=total[:, 1:, :], in0=accs[m][:, 1:, :], in1=block[:, 1:, :], op=ALU.add)
             for jb in range(NB):
                 turn_add(totals[m], jb, total[:, jb, :], False, jb == NB - 1)
 

@@ -59,8 +59,8 @@ def tile_list_interp_gelu_kernel(
         def load_words(dst, src):
             nc.sync.dma_start(out=dst[:], in_=src[0].rearrange("p n t -> p (n t)").bitcast(I32))
 
-        def load_scales(queue, dst, src, r):
-            queue.dma_start(out=dst[r:P:32, :], in_=src[0].bitcast(I32)[r:16:4, :])
+        def load_scales(queue, dst, src, r, first=0):
+            queue.dma_start(out=dst[first + r : P : 32, :], in_=src[0].bitcast(I32)[r:16:4, :])
 
         def load_vector(queue, i, vec):
             queue.dma_start(out=rows[i * NB : (i + 1) * NB, :], in_=vec.rearrange("(c p) -> c p", p=P))
@@ -73,8 +73,8 @@ def tile_list_interp_gelu_kernel(
             )
             return chunk
 
-        nc.sync.dma_start(offsets[:], offs)
         load_words(w_w, w_words)
+        nc.sync.dma_start(offsets[:], offs)
         for r in range(4):
             load_scales(nc.sync if r < 3 else nc.scalar, tab_s, tab_scales, r)
         load_vector(nc.scalar, 2, b)
@@ -83,7 +83,7 @@ def tile_list_interp_gelu_kernel(
         load_vector(nc.sync, 0, iw0)
         load_vector(nc.sync, 1, iw1)
         for r in range(4):
-            load_scales(nc.sync, w_s, w_scales, r)
+            load_scales(nc.sync, w_s, w_scales, r, 4)
         x_raw, wx_pair = [], []
         for a in range(PASSES):
             x_raw.append(load_rows(x, a, 0, J, "x_raw%d" % a))
@@ -133,8 +133,16 @@ def tile_list_interp_gelu_kernel(
         for g in range(2):
             for jb in range(NB):
                 js = slice(g * J + jb * BLK, g * J + (jb + 1) * BLK)
+                if (g, jb) == (0, 0):
+                    for h, i in enumerate((0, NB)):
+                        hs = slice(h * HALF, (h + 1) * HALF)
+                        acc = flat(bank(i))[:, :HALF]
+                        mx(acc, (got_w[:, js], got_s[:, js]), (w_w[:, hs], w_s[4:P, :].bitcast(U8)[:, hs]), True, True)
+                        nc.scalar.activation(out=weighted[0][:, 0, hs], in_=acc, func=ACT.Copy, scale=cols[:, 0:1])
+                    parts.append((0, weighted[0][:, 0, :]))
+                    continue
                 acc = bank(NB + jb)
-                mx(flat(acc), (got_w[:, js], got_s[:, js]), (w_w[:], w_s[:].bitcast(U8)), True, True)
+                mx(flat(acc), (got_w[:, js], got_s[:, js]), (w_w[:], w_s[4:P, :].bitcast(U8)), True, True)
                 if (g, jb) == (1, 0):
                     held = acc
                     continue
@@ -216,8 +224,8 @@ def tile_list_interp_gelu_kernel(
         late = parts[NB:]
         parts = parts[1:NB] + late[:2] + [(0, both[:])] + late[2:]
         totals = [bank(m if m > 0 else 2 * NB - 1) for m in range(NB)]
-        for i, (jb, part) in enumerate(parts):
-            for m in range(TURNED, NB):
+        for m in range(TURNED, NB):
+            for i, (jb, part) in enumerate(parts):
                 turn_add(totals[m], jb, part[:, m * BLK : (m + 1) * BLK], i == 0, i == len(parts) - 1)
 
         first_pair(1)
@@ -237,7 +245,7 @@ def tile_list_interp_gelu_kernel(
 
         add_turned(0)
         multiply(2)
-        early = keep.tile([P, NB, J], F32, name="early", tag="wx_pair1", align_bytes=64)
+        early = keep.tile([P, NB, J], F32, name="early", tag="x_raw1", align_bytes=64)
         for m in range(TURNED, NB):
             nc.scalar.copy(out=early[:, m, :], in_=flat(totals[m]))
         for a in range(PASSES):

@@ -51,7 +51,7 @@ def tile_list_interp_gelu_kernel(
         warm = keep.tile([P, 8], F32, name="warm")
 
         nc.vector.memset(tab_s[:], 0)
-        nc.vector.memset(rows[:], 0.0)
+        nc.gpsimd.memset(rows[:], 0.0)
         nc.vector.memset(w_s[:], 0)
         nc.vector.memset(warm[:, 4:8], 0.0)
         make_identity(nc, ident[:])
@@ -73,11 +73,11 @@ def tile_list_interp_gelu_kernel(
             )
             return chunk
 
+        load_vector(nc.scalar, 2, b)
         load_words(w_w, w_words)
         nc.sync.dma_start(offsets[:], offs)
         for r in range(4):
-            load_scales(nc.sync if r < 3 else nc.scalar, tab_s, tab_scales, r)
-        load_vector(nc.scalar, 2, b)
+            load_scales(nc.sync if r < 2 else nc.scalar, tab_s, tab_scales, r)
         nc.scalar.activation(out=warm[:, 0:1], in_=warm[:, 4:5], func=ACT.Gelu_apprx_tanh)
         load_words(tab_w, tab_words)
         load_vector(nc.sync, 0, iw0)

@@ -95,11 +95,8 @@ def tile_list_interp_gelu_kernel(
         got_s = keep.tile([P, 2 * J], U8, name="got_s", align_bytes=64)
         got_w = keep.tile([P, 2 * J], U32, name="got_w", align_bytes=64)
         nc.vector.tensor_copy(got_s[:], tab_s[:].bitcast(U8).indirect(offsets[:]))
-        for i in range(2 * J // HALF):
-            nc.vector.tensor_copy(
-                got_w[:, i * HALF : (i + 1) * HALF],
-                tab_w[:].bitcast(U32).indirect(offsets[:, i * HALF // 16 : (i + 1) * HALF // 16]),
-            )
+        for lo, hi in ((0, BLK), (BLK, HALF), (HALF, J), (J, 2 * J)):
+            nc.vector.tensor_copy(got_w[:, lo:hi], tab_w[:].bitcast(U32).indirect(offsets[:, lo // 16 : hi // 16]))
 
         turned = bank(NB - 1)
         nc.tensor.transpose(turned[:, 0, :], rows[:], ident[:])

from contextlib import ExitStack

import concourse.mybir as mybir
from concourse.masks import make_identity

K, L, N, T, J = 512, 1024, 512, 2048, 512
FLOPS = 2 * N * J * (2 * K + L)

F32 = mybir.dt.float32
BF16 = mybir.dt.bfloat16
I32 = mybir.dt.int32
U32 = mybir.dt.uint32
U16 = mybir.dt.uint16
U8 = mybir.dt.uint8
FP8X4 = mybir.dt.float8_e4m3fn_x4
ACT = mybir.ActivationFunctionType
ALU = mybir.AluOpType

P = 128
PACK = 4
K_PASS = P * PACK
PASSES = L // K_PASS
BLK = 128
NB = 4
HALF = 256
TURNED = 1


def tile_list_interp_gelu_kernel(
    tc, tab_words, tab_scales, w_words, w_scales, x, wx, iw0, iw1, b, offs, out
):
    nc = tc.nc
    with ExitStack() as ctx:
        keep = ctx.enter_context(tc.tile_pool(name="keep", bufs=1))
        psum = ctx.enter_context(tc.psum_pool(name="psum", bufs=1))

        def bank(i):
            return psum.tile([P, NB, BLK], F32, name="bank%d" % i)

        def flat(tile):
            return tile[:].rearrange("p c n -> p (c n)")

        offsets = keep.tile([P, 2 * J // 16], U16, name="offsets")
        tab_w = keep.tile([P, T], I32, name="tab_w", align_bytes=64)
        tab_s = keep.tile([P, T // 4], I32, name="tab_s", align_bytes=64)
        w_w = keep.tile([P, N], I32, name="w_w", align_bytes=64)
        w_s = keep.tile([P, N // 4], I32, name="w_s", align_bytes=64)
        rows = keep.tile([P, P], F32, name="rows")
        cols = keep.tile([P, 3 * NB], F32, name="cols")
        ident = keep.tile([P, P], F32, name="ident")
        warm = keep.tile([P, 8], F32, name="warm")

        nc.vector.memset(tab_s[:], 0)
        nc.gpsimd.memset(rows[:], 0.0)
        nc.vector.memset(w_s[:], 0)
        nc.vector.memset(warm[:, 4:8], 0.0)
        make_identity(nc, ident[:])

        def load_words(dst, src):
            nc.sync.dma_start(out=dst[:], in_=src[0].rearrange("p n t -> p (n t)").bitcast(I32))

        def load_scales(queue, dst, src, r, first=0):
            queue.dma_start(out=dst[first + r : P : 32, :], in_=src[0].bitcast(I32)[r:16:4, :])

        def load_vector(queue, i, vec):
            queue.dma_start(out=rows[i * NB : (i + 1) * NB, :], in_=vec.rearrange("(c p) -> c p", p=P))

        def load_rows(src, a, first, width, name):
            chunk = keep.tile([P, PACK, width], F32, name=name, align_bytes=64)
            nc.sync.dma_start(
                out=chunk[:],
                in_=src[a * K_PASS : (a + 1) * K_PASS, first : first + width].rearrange("(p t) c -> p t c", t=PACK),
            )
            return chunk

        load_vector(nc.scalar, 2, b)
        load_words(w_w, w_words)
        nc.sync.dma_start(offsets[:], offs)
        for r in range(4):
            load_scales(nc.sync if r < 2 else nc.scalar, tab_s, tab_scales, r)
        nc.scalar.activation(out=warm[:, 0:1], in_=warm[:, 4:5], func=ACT.Gelu_apprx_tanh)
        load_words(tab_w, tab_words)
        load_vector(nc.sync, 0, iw0)
        load_vector(nc.sync, 1, iw1)
        for r in range(4):
            load_scales(nc.sync, w_s, w_scales, r, 4)
        x_raw, wx_pair = [], []
        for a in range(PASSES):
            x_raw.append(load_rows(x, a, 0, J, "x_raw%d" % a))
            wx_pair.append(load_rows(wx, a, 0, HALF, "wx_pair%d" % a))
        wx_raw = [[wx_pair[a][:, :, m * BLK : (m + 1) * BLK] for a in range(PASSES)] for m in range(2)]
        for m in range(2, NB):
            wx_raw.append([load_rows(wx, a, m * BLK, BLK, "wx_raw%d%d" % (m, a))[:] for a in range(PASSES)])

        got_s = keep.tile([P, 2 * J], U8, name="got_s", align_bytes=64)
        got_w = keep.tile([P, 2 * J], U32, name="got_w", align_bytes=64)
        nc.vector.tensor_copy(got_s[:], tab_s[:].bitcast(U8).indirect(offsets[:]))
        for lo, hi in ((0, BLK), (BLK, HALF), (HALF, J), (J, 2 * J)):
            nc.vector.tensor_copy(got_w[:, lo:hi], tab_w[:].bitcast(U32).indirect(offsets[:, lo // 16 : hi // 16]))

        turned = bank(NB - 1)
        nc.tensor.transpose(turned[:, 0, :], rows[:], ident[:])
        nc.scalar.copy(out=cols[:], in_=turned[:, 0, 0 : 3 * NB])

        def cast(copy, grouped, src):
            copy(
                out=grouped.rearrange("p (c i) t -> p c t i", i=4),
                in_=src.rearrange("p t (c i) -> p c t i", i=4),
            )

        def quantize(codes, scales, grouped):
            nc.vector.quantize_mx(out=codes.bitcast(FP8X4), scales=scales, in_=grouped)

        def mx(acc, stat, mov, start, stop):
            nc.tensor.matmul_mx(
                out=acc,
                lhsT=stat[0].bitcast(FP8X4),
                lhsT_scale=stat[1],
                rhs=mov[0].bitcast(FP8X4),
                rhs_scale=mov[1],
                start=start,
                stop=stop,
            )

        def turn_add(total, jb, part, start, stop):
            nc.tensor.matmul(total[:, jb, :], lhsT=part, rhs=ident[:], is_transpose=True, start=start, stop=stop)

        parts = []
        weighted = [keep.tile([P, NB, N], F32, name="weighted%d" % g) for g in range(2)]
        for g in range(2):
            for jb in range(NB):
                js = slice(g * J + jb * BLK, g * J + (jb + 1) * BLK)
                if (g, jb) == (0, 0):
                    for h, i in enumerate((0, NB)):
                        hs = slice(h * HALF, (h + 1) * HALF)
                        acc = flat(bank(i))[:, :HALF]
                        mx(acc, (got_w[:, js], got_s[:, js]), (w_w[:, hs], w_s[4:P, :].bitcast(U8)[:, hs]), True, True)
                        nc.scalar.activation(out=weighted[0][:, 0, hs], in_=acc, func=ACT.Copy, scale=cols[:, 0:1])
                    parts.append((0, weighted[0][:, 0, :]))
                    continue
                acc = bank(NB + jb)
                mx(flat(acc), (got_w[:, js], got_s[:, js]), (w_w[:], w_s[4:P, :].bitcast(U8)), True, True)
                if (g, jb) == (1, 0):
                    held = acc
                    continue
                part = weighted[g][:, jb, :]
                nc.scalar.activation(
                    out=part, in_=flat(acc), func=ACT.Copy, scale=cols[:, g * NB + jb : g * NB + jb + 1]
                )
                parts.append((jb, part))

        def combine():
            both = keep.tile([P, N], F32, name="both", tag="wx_pair0", align_bytes=64)
            nc.vector.scalar_tensor_tensor(
                out=both[:],
                in0=flat(held),
                scalar=cols[:, NB : NB + 1],
                in1=parts[0][1],
                op0=ALU.mult,
                op1=ALU.add,
            )
            return both


        x_q = []

        def quantize_x(a):
            codes = keep.tile([P, J], U32, name="x_codes%d" % a, align_bytes=64)
            scales = keep.tile([P, J], U8, name="x_scales%d" % a, align_bytes=64)
            halves = []
            for h in range(2):
                halves.append(keep.tile([P, HALF, PACK], BF16, name="x_g%d%d" % (a, h), align_bytes=64))
                cast(nc.scalar.copy if (a, h) == (1, 1) else nc.vector.tensor_copy, halves[h][:], x_raw[a][:, :, h * HALF : (h + 1) * HALF])
            for h in range(2):
                hs = slice(h * HALF, (h + 1) * HALF)
                quantize(codes[:, hs], scales[:, hs], halves[h][:].rearrange("p c t -> p (c t)"))
            x_q.append((codes, scales))

        def finish(m, src, js, name, tag):
            res = keep.tile([P, js.stop - js.start], F32, name=name, tag=tag, align_bytes=64)
            nc.scalar.activation(
                out=res[:], in_=src, func=ACT.Gelu_apprx_tanh, bias=cols[:, 2 * NB + m : 2 * NB + m + 1]
            )
            nc.sync.dma_start(out=out[m * BLK : (m + 1) * BLK, js], in_=res[:])

        def acc_bank(m):
            return bank((5, 6, 4, 0)[m])
        last = NB - 1
        grouped = [keep.tile([P, PASSES, BLK, PACK], BF16, name="wx_g%d" % m, align_bytes=64) for m in range(NB)]
        accs = {m: acc_bank(m) for m in (0, 1, 3)}
        on_scalar = ((1, 1), (3, 0))

        def cast_wx(m, a):
            cast(nc.scalar.copy if (m, a) in on_scalar else nc.vector.tensor_copy, grouped[m][:, a, :, :], wx_raw[m][a])

        def multiply(m, passes=range(PASSES)):
            name = "wx%d%d" % (m, passes.start)
            codes = keep.tile([P, len(passes), BLK], U32, name=name + "_codes", align_bytes=64)
            scales = keep.tile([P, len(passes), BLK], U8, name=name + "_scales", align_bytes=64)
            source = grouped[m][:, passes.start : passes.stop, :, :]
            quantize(flat(codes), flat(scales), source.rearrange("p a c t -> p (a c t)"))
            wq = {a: (codes[:, i, :], scales[:, i, :]) for i, a in enumerate(passes)}
            for jb in range(NB if m < TURNED else 0):
                js = slice(jb * BLK, (jb + 1) * BLK)
                for a in passes:
                    first, final = (a, jb) == (0, 0), (a, jb) == (PASSES - 1, NB - 1)
                    mx(accs[m][:, jb, :], (x_q[a][0][:, js], x_q[a][1][:, js]), wq[a], first, final)
            for a in passes if m >= TURNED else []:
                mx(flat(accs[m]), wq[a], (x_q[a][0][:], x_q[a][1][:]), a == 0, a == PASSES - 1)

        def first_pair(a):
            quantize_x(a)
            for m in range(2):
                cast_wx(m, a)
            for m in range(2):
                multiply(m, range(a, a + 1))

        first_pair(0)
        both = combine()
        accs[2] = acc_bank(2)
        late = parts[NB:]
        parts = parts[1:NB] + late[:2] + [(0, both[:])] + late[2:]
        totals = [bank(m if m > 0 else 2 * NB - 1) for m in range(NB)]
        for m in range(TURNED, NB):
            for i, (jb, part) in enumerate(parts):
                turn_add(totals[m], jb, part[:, m * BLK : (m + 1) * BLK], i == 0, i == len(parts) - 1)

        first_pair(1)
        for jb, part in late:
            turn_add(totals[0], jb, part[:, :BLK], jb == 1, False)
        for a in range(PASSES):
            cast_wx(2, a)

        def add_turned(m):
            total = keep.tile([P, NB, BLK], F32, name="turned_sum%d" % m)
            block = weighted[0][:, :, m * BLK : (m + 1) * BLK]
            first = both[:, m * BLK : (m + 1) * BLK]
            nc.vector.tensor_tensor(out=total[:, 0, :], in0=accs[m][:, 0, :], in1=first, op=ALU.add)
            nc.vector.tensor_tensor(out=total[:, 1:, :], in0=accs[m][:, 1:, :], in1=block[:, 1:, :], op=ALU.add)
            for jb in range(NB):
                turn_add(totals[m], jb, total[:, jb, :], False, jb == NB - 1)

        add_turned(0)
        multiply(2)
        early = keep.tile([P, NB, J], F32, name="early", tag="x_raw1", align_bytes=64)
        for m in range(TURNED, NB):
            nc.scalar.copy(out=early[:, m, :], in_=flat(totals[m]))
        for a in range(PASSES):
            cast_wx(last, a)

        def add_early(m, j0, j1):
            js = slice(j0, j1)
            total = keep.tile([P, j1 - j0], F32, name="sum%d_%d" % (m, j0))
            nc.vector.tensor_tensor(out=total[:], in0=flat(accs[m])[:, js], in1=early[:, m, js], op=ALU.add)
            finish(m, total[:], js, "res%d_%d" % (m, j0), "res%d_%d" % (m, j0))

        add_early(1, 0, J)
        finish(0, flat(totals[0]), slice(0, J), "res0", "res0")
        multiply(last, range(0, 1))
        multiply(last, range(1, 2))
        add_early(2, 0, HALF)
        add_early(2, HALF, J)
        add_early(last, 0, HALF)
        add_early(last, HALF, J - BLK)
        add_early(last, J - BLK, J)
